import numpy as np, ml_dtypes
CORES = [5,29,101,125,133,157,229,253]
N = 8
BF = ml_dtypes.bfloat16
V, M, E, RO, LINKS = 1792, 896, 128, 3, 7
GR = np.arange(8)
def pairs(s):
    o = np.argsort(-s, axis=2, kind="stable")
    b = np.stack([np.sum(s > 15 - c, axis=2) for c in range(16)], 2) >> 1
    e = np.concatenate([b[:, :, 1:], np.full_like(b[:, :, :1], M)], 2)
    t = np.arange(M); j = np.sum(b[:, :, :, None] <= t, axis=2) - 1
    bt = np.take_along_axis(b, j, 2); h = np.take_along_axis(e, j, 2) - bt
    return np.take_along_axis(o, bt + t, 2), np.take_along_axis(o, bt + t + h, 2), t - bt, h
def pick(a, ix):
    return np.take_along_axis(a, ix[:, :, None, :], 3)
def swap(a):
    z = a.copy()
    for r in range(LINKS):
        q = (r + 1) % N
        z[r, ..., V - E:] = a[q, ..., :E]; z[q, ..., :E] = a[r, ..., V - E:]
    return z
def pool(rng, m):
    return np.stack([rng.choice(2 ** 20 - 1, m, replace=False) + 1 for g in range(8)])
def boards(rng):
    close = rng.choice(np.array([0, 60, 99, 100, 101, 190]), (N, 8, 1, V)) + (rng.random((N, 8, 16, V)) * rng.choice(np.array([1, 3, 8, 11]), (N, 8, 1, V))).astype(np.int64)
    return np.where(rng.random((N, 8, 1, V)) < 0.4, rng.integers(0, 201, (N, 8, 16, V)), close)
def scores(rng):
    w = rng.choice(np.array([0.5, 1.0, 2.0]), (N, 8, 1))
    return np.minimum((4 * rng.random((N, 8, V)) ** w).astype(np.int64), 3)
def clubs(rng, m):
    a = pool(rng, int(np.max(m)))
    n = a[GR[:, None], (rng.random((N, 8, V)) * m[:, None]).astype(np.int64)]
    p = a[GR[:, None, None], (rng.random((N, 8, 16, V)) * m[:, None, None]).astype(np.int64)]
    return n, np.where(np.arange(16)[:, None] < rng.integers(0, 25, (N, 8, 1, V)), p, 0)
def plant(rng, p, who, name, mask):
    w = np.ascontiguousarray(p).reshape(N, 8, 16 * V); ix = rng.integers(0, 16, who.shape) * V + who
    np.put_along_axis(w, ix, np.where(mask, name, np.take_along_axis(w, ix, 2)), 2)
    return w.reshape(N, 8, 16, V)
def pack(v, p, n, s):
    return {"x": np.ascontiguousarray(v.reshape(N, 128, V)).astype(np.float32).astype(BF), "hi": np.ascontiguousarray(p.reshape(N, 128, V)).astype(np.int32),
            "nm": np.ascontiguousarray(n).astype(np.int32), "sc": np.ascontiguousarray(s).astype(np.int32)}
def setup_inputs(rng):
    n, p = clubs(rng, rng.permutation(np.array([40, 80, 120, 160, 240, 320, 480, 640])))
    return pack(boards(rng), p, n, scores(rng))
def setup_inputs_ends(rng):
    q = V // 4
    cs = [(V, 0, 0, 0), (0, 0, V, 0), (1, 1, 1, V - 3), (V - 3, 1, 1, 1), (0, 1, V - 2, 1), (1, 0, V - 1, 0), (2, 0, V - 5, 3), (q + 1, q - 1, q + 1, q - 1),
          (0, 0, 0, V), (q + 1, 0, 0, V - q - 1), (0, V, 0, 0), (1, 0, 0, V - 1), (0, 0, 1, V - 1), (1, V - 2, 0, 1), (0, q - 1, 0, V - q + 1), (V - 3, 0, 0, 3)]
    s = np.zeros((N, 8, V), np.int64)
    for r in range(N):
        o = rng.permutation(16)[:8] if r > 1 else 8 * r + np.arange(8)
        for g in range(8): s[r, g] = rng.permutation(np.repeat(np.array([3, 2, 1, 0]), cs[int(o[g])]))
    n, p = clubs(rng, rng.permutation(np.array([40, 80, 120, 160, 240, 320, 480, 640])))
    return pack(boards(rng), p, n, s)
def setup_inputs_met(rng):
    s = scores(rng); a = pool(rng, N * V); n = np.ascontiguousarray(a.reshape(8, N, V).transpose(1, 0, 2))
    s[:2, 7] = rng.integers(0, 4, (2, 1))
    for r in (2, 3): s[r, 6] = rng.permutation(np.repeat(np.array([3, 2, 1, 0]), (4, 4, 4, V - 12)))
    p = a[GR[:, None, None], rng.integers(0, N * V, (N, 8, 16, V))]
    U, L, i, h = pairs(s); nu, nl = np.take_along_axis(n, U, 2), np.take_along_axis(n, L, 2)
    for r in (2, 3): p[r, 6][:, U[r, 6, 0:6:2]] = 0
    share = rng.choice(np.array([0.0, 0.02, 0.1, 0.3, 0.5, 0.9, 1.0]), (N, 8, 1)); share[0, :, 0] = (0.0, 0.02, 0.1, 0.3, 0.5, 0.7, 0.9, 1.0); share[1, 7] = 1.0
    again = (rng.random((N, 8, M)) < share) | ((i == h - 1) & (h % 2 == 1)); again[2:4, 6, :6] = np.arange(6) % 2 == 1
    p = plant(rng, p, L, nu, rng.random((N, 8, M)) < 0.3)
    p = plant(rng, p, U, np.roll(nl, -1, 2), rng.random((N, 8, M)) < 0.1)
    p = plant(rng, p, U, nl, again)
    return pack(boards(rng), p, n, s)
def setup_inputs_ties(rng):
    v = boards(rng); kind = rng.integers(0, 2, (N, 1, V)); row = np.arange(16)[:, None]
    v[:, 0] = 100
    v[:, 1] = np.where((row < 8) == (kind == 1), 150, 50)
    v[:, 2] = 200 * rng.integers(0, 2, (N, 16, V))
    v[:, 3] = 100 + (row == rng.integers(0, 16, (N, 1, V)))
    v[:, 4] = 100 + rng.integers(0, 2, (N, 16, V))
    v[:, 5] = np.where(kind == 1, 200, 0)
    n, p = clubs(rng, rng.permutation(np.array([40, 80, 120, 160, 240, 320, 480, 640])))
    s = scores(rng); s[:, 0] = np.where(np.arange(N)[:, None] % 2 == 0, rng.integers(0, 4, (N, 1)), s[:, 0])
    return pack(v, p, n, s)
def setup_inputs_alike(rng):
    n, p = clubs(rng, np.array([1, 1, 2, 3, 5, 17, 17, 400]))
    p[:, 1] = 0; p[:, 3] = 0; p[:, 5] = p[:, 5, :1].copy(); p[:, 6, :15] = 0
    n[:, 2] = np.where(rng.random((N, V)) < 0.5, 1, 2 ** 20 - 1); p[:, 2] = rng.choice(np.array([0, 1, 2 ** 20 - 1]), (N, 16, V))
    n[:, 3] = rng.integers(1, 4, (N, V))
    n[:, 7] = 2 ** 20 - 1 - rng.integers(0, 3, (N, V)); p[:, 7] = rng.integers(0, 3, (N, 16, V))
    return pack(boards(rng), p, n, scores(rng))
def setup_inputs_spread(rng):
    v = np.minimum((np.exp2(8 * rng.random((N, 8, 1, V))) * rng.random((N, 8, 16, V))).astype(np.int64), 200)
    n = np.minimum(np.exp2(20 * rng.random((N, 8, V))).astype(np.int64), 2 ** 20 - 1)
    p = np.minimum(np.exp2(20 * rng.random((N, 8, 16, V))).astype(np.int64), 2 ** 20 - 1) * (rng.random((N, 8, 16, V)) > 0.0625)
    n[:, 7] = 2 ** 20 - 1 - rng.integers(0, 200, (N, V)); p[:, 7] = 2 ** 20 - 1 - rng.integers(0, 200, (N, 16, V))
    return pack(v, p, n, np.minimum((4 * rng.random((N, 8, V)) ** 4).astype(np.int64), 3))
def check_inputs(d):
    bad = []
    for k, lo, hi_ in (("x", 0, 200), ("hi", 0, 2 ** 20 - 1), ("nm", 1, 2 ** 20 - 1), ("sc", 0, 3)):
        a = np.asarray(d[k]).astype(np.float64)
        if not np.all((a >= lo) & (a <= hi_)): bad.append("range of " + k)
        elif not np.all(a == np.floor(a)): bad.append("whole numbers in " + k)
    return bad
def reference(x, hi, nm, sc):
    v = x.astype(np.float32).astype(np.int32).reshape(N, 8, 16, V); p = hi.astype(np.int32).reshape(N, 8, 16, V)
    n = nm.astype(np.int32); s = sc.astype(np.int32)
    for rnd in range(RO):
        U, L, i, h = pairs(s)
        pu = pick(p, U)
        met = np.any(pu == np.take_along_axis(n, L, 2)[:, :, None, :], axis=2)
        ex = ((i & 1) == 0) & (i + 1 < h) & (met | np.roll(met, -1, 2))
        L = np.where(ex, np.roll(L, -1, 2), np.where(np.roll(ex, 1, 2), np.roll(L, 1, 2), L))
        xu, xl, pl = pick(v, U), pick(v, L), pick(p, L)
        nu, nl = np.take_along_axis(n, U, 2), np.take_along_axis(n, L, 2)
        wu, wl = np.sum(xu > xl, axis=2), np.sum(xl > xu, axis=2)
        su = np.take_along_axis(s, U, 2) + 2 * (wu > wl) + (wu == wl); sl = np.take_along_axis(s, L, 2) + 2 * (wl > wu) + (wu == wl)
        v = swap(np.concatenate([xu + (xl > xu), xl + (xu > xl)], 3))
        p = swap(np.concatenate([np.concatenate([nl[:, :, None, :], pu[:, :, :15]], 2), np.concatenate([nu[:, :, None, :], pl[:, :, :15]], 2)], 3))
        n = swap(np.concatenate([nu, nl], 2)); s = swap(np.concatenate([su, sl], 2))
    return {"yx": v.reshape(N, 128, V).astype(np.float32).astype(BF), "yn": n.astype(np.float32), "ys": s.astype(np.float32)}

@@ -1,0 +1,638 @@
+from concourse.bass import DstId, RemoteDMATransfer
+from concourse.mybir import AluOpType as ALU, ActivationFunctionType as AF
+
+V, M, E, RO = 1792, 896, 128, 3
+F, B, H, I, U = "float32", "bfloat16", "float16", "int32", "uint16"
+SCRATCH = {}
+
+
+def _sb(name, cols, dt):
+    SCRATCH[name] = ("sbuf", [128, cols], dt)
+
+
+for _r in range(4):
+    _sb("X%d" % _r, 2048, B)
+    _sb("N%d" % _r, 2048, F)
+for _r in range(3):
+    _sb("H%d" % _r, 2048, F)
+    _sb("WV%d" % _r, V, F)
+    _sb("WS%d" % _r, V, F)
+    _sb("SI%d" % _r, 256, B)
+    _sb("AI%d" % _r, 256, B)
+for _n, _c, _d in [
+        ("Hi", V, I), ("P0", V, F), ("P1", V, F), ("sci", 112, I), ("nmi", 112, I), ("nmf", 112, F),
+        ("zer", 112, F), ("zr2", 112, F), ("one", 112, B), ("m256", 8, B), ("cA", 32, B), ("cB", 8, B),
+        ("J", 144, F), ("D0", 128, F), ("pc", 8, I), ("pa", 8, I), ("col", 16, F), ("ta", 144, F),
+        ("le", 16, F), ("ge", 16, F),
+        ("ON", 128, B), ("Oh", 128, B), ("On", 128, B), ("Om", 128, B), ("oa", 128, B), ("ob", 128, B),
+        ("LT", 128, B), ("UT", 128, B), ("Ib", 128, B), ("In", 128, B), ("Ik", 128, B), ("I28", 128, B),
+        ("Z", 144, B), ("Zn", 144, B), ("Za", 144, B), ("Z2", 144, B), ("Z3", 144, B),
+        ("Ih", 128, H), ("Is", 128, H), ("SH", 128, H), ("W1", 128, H), ("IU", 128, H), ("W2", 128, H),
+        ("h1", 128, H), ("h2", 128, H),
+        ("tau0", 112, F), ("tau", 112, F), ("taur", 256, F), ("tr", 64, F), ("t2", 64, F), ("th", 64, F),
+        ("Ec", 896, B), ("Cc", 896, B), ("Mc", 896, H), ("Y", 896, H), ("Ys", 896, B), ("q16", 112, H),
+        ("bb", 32, F), ("td", 16, F), ("th2", 8, F),
+        ("fi", 112, I), ("fu", 112, F), ("fw", 112, F), ("OFF", 112, U),
+        ("wv", 112, F), ("ws", 112, F), ("mx", 112, F), ("UL", 112, U), ("ORD", 112, H),
+        ("Pj", 512, H), ("Oj", 896, B), ("A", 256, B), ("zi", 64, I), ("za", 64, I), ("thr", 64, F),
+        ("Nl", 944, F), ("EQ", 944, B), ("ex", 64, H), ("Dd", 64, H), ("LP", 56, U),
+        ("Xu", M, B), ("Dx", M, B), ("Sg", M, B), ("Gt", M, B), ("cl", 112, B), ("sp", 112, B), ("so", 112, F)]:
+    _sb(_n, _c, _d)
+SCRATCH["nd"] = ("dram", [8, V], F)
+PSUM = ["pA", "pB", "pC", "pE", "pG", "p0", "p1", "p2"]
+for _n in PSUM:
+    SCRATCH[_n] = ("psum", [128, 512], F)
+
+KINDS = ["A", "S", "X", "N", "H"]
+SEMAPHORES = ["qv", "qs", "qt", "qg", "lsc", "lnm", "lx", "lh", "lnd", "lN", "o1", "o2", "o3", "o4", "o5", "o6", "o7"]
+for _r in range(RO):
+    SEMAPHORES += ["wv%d" % _r, "ws%d" % _r, "ie%d" % _r, "im%d" % _r, "lz%d" % _r]
+    for _k in KINDS:
+        SEMAPHORES += ["a%s%d" % (_k, _r), "l%s%d" % (_k, _r)]
+
+MAGIC = 12582912.0
+OFFS = 32.0
+BIG = 4096.0
+KV = [56, 56, 56]
+OS = [0, 2, 3]
+HS = 768
+
+
+def pieces(kind, r):
+    if kind == "A":
+        return ("A", 128, 0, "AI%d" % r, 128, 0)
+    if kind == "S":
+        return ("Sg", 128, 0, "SI%d" % r, 128, 0)
+    n = "%s%d" % (kind, r + 1)
+    return (n, 128, 1792, n, 1920, 0)
+
+
+def relays(T, topo, rank):
+    core = T.cores[rank]
+    out, used = {}, []
+    for d, nb in ((0, rank - 1), (1, rank + 1)):
+        if nb < 0 or nb >= len(T.cores):
+            continue
+        ok = [c for c in topo.cores_of(core) if c != core and c not in used and topo.may_write(c, T.cores[nb])]
+        near = [c for c in ok if topo.die(c) == topo.die(core)][0]
+        far = [c for c in ok if topo.die(c) != topo.die(core)][0]
+        used += [near, far]
+        out[d] = (near, far)
+    return out
+
+
+def relay_of(kind, pair):
+    return pair[0] if kind in ("A", "S", "X") else pair[1]
+
+
+def half_mask(topo, src, dst, d):
+    e = topo.engines(src, dst)
+    h = len(e) // 2
+    return sum(1 << x for x in (e[:h] if d == 0 else e[h:])), h
+
+
+def relay_program(g, core, T, topo):
+    for rank in range(len(T.cores)):
+        for d, pair in relays(T, topo, rank).items():
+            if core not in pair:
+                continue
+            dst = T.cores[rank - 1 if d == 0 else rank + 1]
+            rid, pid = topo.addr(dst, core)
+            n_in = half_mask(topo, T.cores[rank], core, d)[1]
+            n_out = len(topo.engines(core, dst))
+            done = []
+            for r in range(RO):
+                for k in KINDS:
+                    if relay_of(k, pair) != core or (k == "H" and r == RO - 1):
+                        continue
+                    p = pieces(k, r)
+                    ap = T[p[3]][:, p[4 + d]:p[4 + d] + E]
+                    g.wait_ge(T.sem["a%s%d" % (k, r)], n_in)
+                    g.remote_dma(ap, ap, T.sem["a%s%d" % (k, r)], T.sem["l%s%d" % (k, r)], pid, rid, topo.mask(core, dst))
+                    done.append("l%s%d" % (k, r))
+            for s in done:
+                g.wait_ge(T.sem[s], n_out)
+
+
+def rank_program(g, core, T, topo):
+    rank = T.rank_of(core)
+    if rank is None:
+        relay_program(g, core, T, topo)
+        return
+    prev, nxt = rank > 0, rank < len(T.cores) - 1
+    rel = relays(T, topo, rank)
+    ops = []
+
+    def R(name, a, b, step=None, row=None):
+        t = T[name]
+        if row is not None:
+            ap = t[row:128:16, a:b]
+        elif step is not None:
+            ap = t[:, a:b:step]
+        else:
+            ap = t[:, a:b]
+        return (ap, [(name, a, b)], [])
+
+    def IND(win, off):
+        return (win[0].indirect(off[0]), win[1], off[1])
+
+    def EXT(ap):
+        return (ap, [], [])
+
+    def add(q, fn, outs, ins, sem=None, inc=16):
+        rd, wr = [], []
+        for o in outs:
+            wr += o[1]
+            rd += o[2]
+        for x in ins:
+            if isinstance(x, tuple):
+                rd += x[1] + x[2]
+        ops.append({"q": q, "fn": fn, "rd": rd, "wr": wr, "sem": sem, "inc": inc})
+
+    def val(x):
+        return x[0] if isinstance(x, tuple) else x
+
+    def fill(out, c):
+        add("v", lambda: g.vector.memset(out[0], c), [out], [])
+
+    def ts(out, a, s1, op0, s2=None, op1=None):
+        if op1 is None:
+            add("v", lambda: g.vector.tensor_scalar(out[0], a[0], val(s1), None, op0), [out], [a, s1])
+        else:
+            add("v", lambda: g.vector.tensor_scalar(out[0], a[0], val(s1), val(s2), op0, op1), [out], [a, s1, s2])
+
+    def tt(out, a, b, op):
+        add("v", lambda: g.vector.tensor_tensor(out[0], a[0], b[0], op), [out], [a, b])
+
+    def cp(out, a):
+        add("v", lambda: g.vector.tensor_copy(out[0], a[0]), [out], [a])
+
+    def act(out, a, func, bias=None, scale=None):
+        kw = {}
+        if bias is not None:
+            kw["bias"] = val(bias)
+        if scale is not None:
+            kw["scale"] = val(scale)
+        add("s", lambda: g.scalar.activation(out[0], a[0], func, **kw), [out], [a, bias, scale])
+
+    def lin(out, a, scale, bias):
+        act(out, a, AF.Identity, bias=bias, scale=scale)
+
+    def group(items, start=True, stop=True):
+        for n, (out, l, rr) in enumerate(items):
+            add("t", lambda out=out, l=l, rr=rr, n=n: g.tensor.matmul(out[0], l[0], rr[0], start and n == 0,
+                                                                      stop and n == len(items) - 1), [out], [l, rr])
+
+    def iota(out, pat, base, cm, isint=False):
+        if isint:
+            add("g", lambda: g.iota(out[0], pat, base, cm), [out], [])
+        else:
+            add("g", lambda: g.iota(out[0], pat, base, cm, allow_small_or_imprecise_dtypes=True), [out], [])
+
+    def dma(q, out, a, sem):
+        eng = g.sync if q == "y" else g.scalar
+        add(q, lambda: eng.dma_start(out[0], a[0]), [out], [a], sem=sem)
+
+    def send(kind, r):
+        p = pieces(kind, r)
+        trs, srcs, tot, got, lands = [], [], 0, 0, []
+        for d in sorted(rel):
+            h = relay_of(kind, rel[d])
+            rid, pid = topo.addr(h, core)
+            m, n = half_mask(topo, core, h, d)
+            s = R(p[0], p[1 + d], p[1 + d] + E)
+            srcs.append(s)
+            trs.append(RemoteDMATransfer(dst_ids=[DstId(rid=rid, pnc=pid)], dma_engine_mask=m, remote_sem=T.sem["a%s%d" % (kind, r)],
+                                         src=s[0], dst=T[p[3]][:, p[4 + d]:p[4 + d] + E]))
+            tot += n
+            nb = rank - 1 if d == 0 else rank + 1
+            far = relay_of(kind, relays(T, topo, nb)[1 - d])
+            got += len(topo.engines(far, core))
+            lands.append(R(p[3], p[5 - d], p[5 - d] + E))
+        ls = "l%s%d" % (kind, r)
+        add("g", lambda: g.remote_dma_fused(trs, local_sem=T.sem[ls]), [], srcs, sem=ls, inc=tot)
+        ops[-1]["own"] = True
+        add("x", None, lands, [], sem="a%s%d" % (kind, r), inc=got)
+
+    def RS(name, i):
+        return R(name, 15 - i, 143 - i)
+
+    def C1(name, j):
+        return R(name, j, j + 1)
+
+    def W(name):
+        return R(name, 0, 128)
+
+    def blk(name, j):
+        return R(name, 112 * j, 112 * j + 112)
+
+    def zero(r):
+        dma("y", R("WV%d" % r, 0, V, row=0), R("zr2" if r else "zer", 0, 112), "lz%d" % r)
+        dma("y", R("WS%d" % r, 0, V, row=0), R("zr2" if r else "zer", 0, 112), "lz%d" % r)
+
+    def sel(out, a, op, c, base, sign=1):
+        add("g", lambda: g.affine_select(T[out][:], T[a][:], [[sign, 128]], op, c, base, -sign), [W(out)], [W(a)])
+
+    def hat(name, c, k):
+        act(R("ta", 0, 144), R("J", 0, 144), AF.Abs, bias=C1("col", c))
+        act(R(name, 0, 144), R("ta", 0, 144), AF.Relu, bias=k, scale=-1.0)
+
+    dma("y", R("sci", 0, 112), EXT(T.sc[:]), "lsc")
+    dma("s", R("nmi", 0, 112), EXT(T.nm[:]), "lnm")
+    fill(R("zer", 0, 112), 0.0)
+    zero(0)
+    dma("y", R("Hi", 0, V), EXT(T.hi[:]), "lh")
+    iota(R("pc", 0, 1), [[1, 1]], 0, 1, True)
+    iota(R("J", 0, 144), [[1, 144]], 0, 0)
+    iota(W("D0"), [[1, 128]], 0, -1)
+    iota(R("cB", 0, 8), [[0, 8]], 56, 0)
+    iota(R("m256", 0, 8), [[0, 8]], -int(BIG) // 16, 0)
+    iota(R("tr", 0, 10), [[16, 10]], 16 * 46, 1)
+    iota(R("tr", 10, 20), [[16, 10]], 0, 1)
+    ts(R("pa", 0, 1), R("pc", 0, 1), 112, ALU.bitwise_and)
+    fill(R("cA", 0, 8), -1.0 / 64)
+    cp(C1("col", 0), R("pa", 0, 1))
+    fill(R("cA", 8, 16), 1.0 / 64)
+    ts(W("oa"), W("J"), C1("col", 0), ALU.subtract, 0.0, ALU.is_ge)
+    ts(W("ob"), W("J"), C1("col", 0), ALU.subtract, 16.0, ALU.is_lt)
+    fill(R("cA", 16, 32), -1.0 / 64)
+    tt(W("ON"), W("oa"), W("ob"), ALU.mult)
+    ts(W("Ib"), W("D0"), 0.0, ALU.is_equal)
+    sel("LT", "ON", ALU.is_gt, 0.0, 0)
+    sel("UT", "ON", ALU.is_gt, 0.0, 0, -1)
+    iota(R("tr", 20, 61), [[16, 41]], 16 * 8, 1)
+    iota(R("P0", 0, V), [[1, 112], [112, 16]], int(OFFS), 0)
+    act(R("zr2", 0, 112), R("J", 0, 112), AF.Silu, scale=0.0)
+    ts(W("Ik"), W("D0"), 0.0, ALU.is_equal, BIG, ALU.mult)
+    ts(W("Ih"), W("D0"), 0.0, ALU.is_equal)
+    ts(W("Is"), W("D0"), 0.0, ALU.is_equal, 0.0625, ALU.mult)
+    cp(R("nmf", 0, 112), R("nmi", 0, 112))
+    ND = (T.nd[:], [("nd", 0, V)], [])
+    lin(W("Oh"), W("ON"), 0.5, 0.0)
+    lin(W("On"), W("ON"), -0.5, 0.0)
+    dma("s", ND, R("nmf", 0, 112), "lnd")
+    for j, sc_, bi_ in ((2, -1.0, -15.0), (3, -1.0, -23.0), (4, -1.0, -15.5), (5, 2.0, -1.0), (6, -1.0, 0.0), (7, -112.0, -895.75)):
+        lin(C1("col", j), C1("col", 0), sc_, bi_)
+    for i in range(16):
+        dma("y", R("N0", 128, 1920, row=i), ND, "lN")
+    dma("y", R("X0", 128, 1920), EXT(T.x[:]), "lx")
+    lin(W("I28"), W("Ib"), -28.0, 0.0)
+    hat("Z", 2, 1.0)
+    lin(W("Om"), W("ON"), -1.0, 0.0)
+    lin(R("t2", 0, 61), R("tr", 0, 61), -2.0, C1("col", 5))
+    lin(R("th", 0, 61), R("tr", 0, 61), 1.0, C1("col", 6))
+    iota(R("taur", 0, 128), [[2, 128]], 2 * 768 + 1, 0)
+    iota(R("taur", 128, 256), [[2, 128]], 0, 0)
+    iota(R("tau", 0, 112), [[1, 112]], 0, 112)
+    sel("h1", "ON", ALU.is_equal, 0.0, -1)
+    sel("W1", "ON", ALU.is_equal, 0.0, 15)
+    sel("SH", "h1", ALU.not_equal, -1.0, 0)
+    sel("h2", "Om", ALU.is_equal, 0.0, 1)
+    sel("W2", "Om", ALU.is_equal, 0.0, -15)
+    sel("IU", "h2", ALU.not_equal, 1.0, 0)
+    iota(R("one", 0, 112), [[0, 112]], 1, 0)
+
+    def places():
+        lo1 = 0 if prev else 128
+        iota(R("P1", 0, V), [[1, 112], [112, 16]], int(OFFS) + 128 - lo1, 0)
+        if prev:
+            iota(R("P1", 0, V, step=16), [[1, 112]], int(OFFS), 0)
+            iota(R("P1", 1, 256, step=16), [[1, 16]], int(OFFS) + 112, 0)
+        if nxt:
+            iota(R("P1", 96 * 16 + 14, V, step=16), [[1, 16]], int(OFFS) + 1664 + 256 - lo1, 0)
+            iota(R("P1", 15, V, step=16), [[1, 112]], int(OFFS) + 1680 + 256 - lo1, 0)
+
+    def rows():
+        tt(C1("col", 1), R("pc", 0, 1), R("pa", 0, 1), ALU.subtract)
+        ts(R("le", 0, 16), R("J", 0, 16), C1("col", 1), ALU.is_ge, BIG, ALU.mult)
+
+    def consts2():
+        lin(R("ge", 1, 16), R("le", 0, 15), -1.0, BIG)
+        lin(C1("col", 8), C1("le", 7), 895.5 / BIG, C1("col", 7))
+        lin(W("In"), W("Ib"), -1.0, 0.0)
+        for j, (a, b, jl, jg) in enumerate(((0, 16, 1, 15), (16, 96, 0, 15), (96, 112, 0, 14))):
+            c_ = C1("col", 8)
+            if prev:
+                lin(C1("col", 9 + j), C1("le", jl), 1.0, c_)
+                c_ = C1("col", 9 + j)
+            if nxt:
+                lin(C1("col", 12 + j), C1("ge", jg), 1.0, c_)
+                c_ = C1("col", 12 + j)
+            lin(R("tau0", a, b), R("tau", a, b), 1.0, c_)
+        lin(R("Zn", 0, 144), R("Z", 0, 144), -1.0, 0.0)
+
+    def up(ps, o, c, n):
+        group([(R(ps, o, o + n), W("Ib"), R("Xu", c, c + n)), (R(ps, o, o + n), W("Ib"), R("Gt", c, c + n))])
+
+    def low(ps, o, c, n):
+        group([(R(ps, o, o + n), W("Ib"), R("Xu", c, c + n)), (R(ps, o, o + n), W("Ib"), R("Dx", c, c + n)),
+               (R(ps, o, o + n), W("In"), R("Sg", c, c + n)), (R(ps, o, o + n), W("Ib"), R("Gt", c, c + n))])
+
+    def gat(dst, c0, win, off, a, b):
+        act(R(dst, c0, c0 + 16 * (b - a)), IND(win, R(off, a, b)), AF.Copy)
+
+    def mets(ps, c0, n, first):
+        it = [(R(ps, 0, n), RS("Z3", i), R("EQ", 16 * c0 + i, 16 * (c0 + n), step=16)) for i in range(15)]
+        if first:
+            it.append((R(ps, 1, n), RS("Z", 0), R("EQ", 15, 16 * (n - 1), step=16)))
+        else:
+            it.append((R(ps, 0, n), RS("Z", 0), R("EQ", 16 * c0 - 1, 16 * (c0 + n - 1), step=16)))
+        it.append((R(ps, 0, n), RS("Z", 15), R("EQ", 16 * c0 + 15, 16 * (c0 + n), step=16)))
+        group(it)
+
+    for r in range(RO):
+        K = 4 + 2 * r
+        last = r == RO - 1
+        lo, hi = (128, 1920) if r == 0 else (0 if prev else 128, 2048 if nxt else 1920)
+        Xc, Xn, Nn, Hn = "X%d" % r, "X%d" % (r + 1), "N%d" % (r + 1), "H%d" % (r + 1)
+        Xw, Nw, Hw = R(Xc, lo, hi), R("N%d" % r, lo, hi), R("H%d" % r, lo, hi)
+        PAY = "P0" if r == 0 else "P1"
+        for j in range(K):
+            k = K - 1 - j
+            if r == 0:
+                ts(blk("Ec", j), R("sci", 0, 112), float(k), ALU.is_equal)
+            else:
+                ts(blk("Ec", j), R("sp", 0, 112), float(k - 1), ALU.is_equal)
+        Wd = 112 * K
+        for ps, a, b in (("p2", 0, K // 2), ("p0", K // 2, K)):
+            group([(R(ps, 0, 112 * (b - a)), W("Ik"), R("Ec", 112 * a, 112 * b))], stop=False)
+        add("v", lambda Wd=Wd: g.vector.tensor_tensor_scan(T.Cc[:, 0:Wd], T.Ec[:, 0:Wd], T.Ec[:, 0:Wd], 0.0, ALU.add, ALU.max),
+            [R("Cc", 0, Wd)], [R("Ec", 0, Wd)])
+        hiK, hiJ = R("Cc", 111, Wd, step=112), R("Cc", 111, Wd - 112, step=112)
+        group([(R("pC", 128, 160), W("ON"), R("cA", 0, 32)), (R("pC", 136, 144), W("ON"), R("cB", 0, 8))], stop=False)
+        group([(R("pB", 0, K), W("ON"), R("m256", 0, K)), (R("pB", 0, K), W("LT"), hiK), (R("pB", 1, K), W("UT"), hiJ)])
+        group([(R("p2", 0, Wd // 2), W("Ib"), R("Cc", 0, Wd // 2))], start=False)
+        group([(R("pC", 128, 128 + K), W("Oh"), hiK), (R("pC", 136, 136 + K), W("On"), hiK),
+               (R("pC", 145, 144 + K), W("Oh"), hiJ), (R("pC", 153, 152 + K), W("Oh"), hiJ)], start=False)
+        group([(R("p0", 0, Wd // 2), W("Ib"), R("Cc", Wd // 2, Wd))], start=False)
+        for j in range(K // 2):
+            ts(blk("Mc", j), blk("p2", j), C1("pB", j), ALU.add, 0.0, ALU.max)
+        ts(R("bb", 0, 32), R("pC", 128, 160), MAGIC, ALU.add, -MAGIC, ALU.add)
+        for j in range(K // 2, K):
+            ts(blk("Mc", j), blk("p0", j - K // 2), C1("pB", j), ALU.add, 0.0, ALU.max)
+        group([(R("pC", 0, 112), W("Ih"), blk("Mc", j)) for j in range(K)])
+        lin(R("th2", 0, 8), R("bb", 0, 8), -2.0, -0.5)
+        tt(R("td", 0, 16), R("bb", 0, 16), R("bb", 16, 32), ALU.add)
+        cp(R("q16", 0, 112), R("pC", 0, 112))
+        ns = K - 1
+        for j in range(ns):
+            act(blk("Ys", j), R("pC", 0, 112), AF.Sign, bias=C1("th2", j))
+        if r == 0:
+            hat("Z3", 4, 1.5)
+            hat("Za", 3, 1.0)
+        for j in range(K):
+            ts(blk("Y", j), R("q16", 0, 112), C1("td", j), ALU.is_gt, C1("td", 8 + j), ALU.mult)
+        it = [(W("Is"), R("q16", 0, 112))]
+        for j in range(K):
+            it.append((W("Is"), blk("Y", j)))
+            if j > 0:
+                it.append((W("I28"), blk("Ys", j - 1)))
+        group([(R("pG", 256, 368), a, b) for a, b in it])
+        group([(R("pE", 64, 65), RS("Z", j), C1("Cc", 112 * j + 111)) for j in range(K - 1)])
+        if r > 0:
+            up("p2", 0, 768, 128)
+            up("p2", 128, 0, 128)
+            low("p2", 256, 128, 256)
+            low("p0", 0, 384, 512)
+        else:
+            rows()
+        ts(R("fi", 0, 112), R("pG", 256, 368), -17.0 / 32.0 - 28.0 * ns, ALU.add)
+        ts(R("fu", 0, 112), R("fi", 0, 112), 1791.0 / 1792.0, ALU.mult, 0.0625 + 28.0 * ns, ALU.add)
+        tt(R("fw", 0, 112), R("pG", 256, 368), R("fu", 0, 112), ALU.subtract)
+        ts(R("OFF", 0, 112), R("fw", 0, 112), 1792.0, ALU.mult, 0.25, ALU.add)
+        kv = KV[r]
+        act(IND(R("WS%d" % r, 0, V), R("OFF", kv, 112)), R(PAY, 16 * kv, V), AF.Silu)
+        cp(IND(R("WV%d" % r, 0, V), R("OFF", 0, kv)), R(PAY, 0, 16 * kv))
+        dma("y", R("wv", 0, 112), R("WV%d" % r, 0, V, row=0), "wv%d" % r)
+        dma("s", R("ws", 0, 112), R("WS%d" % r, 0, V, row=0), "ws%d" % r)
+        if r == 0:
+            consts2()
+        else:
+            if r == 1:
+                act(R(Xc, 256, 768), R("p1", 0, 512), AF.Copy)
+            act(R(Xc, 768, 1280), R("p2", 0, 512), AF.Copy)
+            act(R(Xc, 1280, 1792), R("p0", 0, 512), AF.Copy)
+        ts(R("A", 0, 256), R("taur", 0, 256), C1("pE", 64), ALU.is_lt)
+        send("A", r)
+        if r == 0:
+            places()
+        for j in range(K - 1):
+            ts(R("Pj", 64 * j, 64 * j + 61), R("t2", 0, 61), C1("th2", j), ALU.is_lt, C1("td", 8 + j), ALU.mult)
+        group([(R("pG", 128, 189), W("Ih"), R("Pj", 64 * j, 64 * j + 61)) for j in range(K - 1)])
+        for j in range(OS[r]):
+            ts(blk("Oj", j), R("tau0", 0, 112), C1("pC", 128 + j), ALU.is_lt)
+        if r == 0:
+            tt(R("Z2", 0, 144), R("Za", 0, 144), R("Z", 0, 144), ALU.subtract)
+        tt(R("zi", 0, 61), R("pG", 128, 189), R("th", 0, 61), ALU.add)
+        ts(R("za", 0, 61), R("zi", 0, 61), 1, ALU.bitwise_and)
+        ts(R("thr", 0, 61), R("za", 0, 61), 0.0, ALU.is_equal, 100.0, ALU.mult)
+        if r == 0:
+            cp(R("H0", 128, 128 + HS), R("Hi", 0, HS))
+        tt(R("mx", 0, 112), R("wv", 0, 112), R("ws", 0, 112), ALU.max)
+        ts(R("UL", 0, 112), R("mx", 0, 112), 0.25 - OFFS, ALU.add)
+        ts(R("ORD", 0, 112), R("mx", 0, 112), MAGIC - OFFS, ALU.add, -MAGIC, ALU.add)
+        for (o, a, n) in ((0, 46, 10), (10, 0, 10), (20, 8, 41)):
+            group([(R("pA", 256 + o, 256 + o + n), W("SH"), R("ORD", 56 + a, 56 + a + n)),
+                   (R("pA", 256 + o, 256 + o + n), W("W1"), R("ORD", 55 + a, 55 + a + n))])
+
+        def cmpq(c0, a, b):
+            n = 16 * (b - a)
+            tt(R("EQ", c0, c0 + n), IND(Hw if r else R("Hi", 0, V), R("UL", a, b)), R("Nl", c0, c0 + n), ALU.is_equal)
+
+        gat("Nl", 0, Nw, "UL", 102, 112)
+        gat("Nl", 160, Nw, "UL", 56, 66)
+        gat("Nl", 320, Nw, "UL", 66, 86)
+        gat("Xu", 0, Xw, "UL", 48, 56)
+        gat("Xu", 128, Xw, "UL", 0, 8)
+        gat("Nl", 640, Nw, "UL", 86, 105)
+        cmpq(0, 46, 56)
+        cmpq(160, 0, 10)
+        mets("pE", 0, 20, True)
+        cmpq(320, 10, 30)
+        tt(R("ex", 0, 20), R("pE", 0, 20), R("thr", 0, 20), ALU.is_gt)
+        tt(R("Dd", 0, 20), R("ex", 0, 20), R("pA", 256, 276), ALU.mult)
+        group([(R("pE", 32, 48), W("IU"), R("Dd", 2, 18)), (R("pE", 32, 40), W("Ih"), R("ORD", 104, 112)),
+               (R("pE", 40, 48), W("Ih"), R("ORD", 56, 64)), (R("pE", 32, 48), W("W2"), R("Dd", 3, 19))])
+        cp(R("LP", 0, 16), R("pE", 32, 48))
+        tt(R("Dx", 0, 256), IND(Xw, R("LP", 0, 16)), R("Xu", 0, 256), ALU.subtract)
+        ts(R("Sg", 0, 256), R("Dx", 0, 256), 1.0, ALU.min, -1.0, ALU.max)
+        send("S", r)
+        ts(R("Gt", 0, 256), R("Dx", 0, 256), 0.0, ALU.is_gt)
+        up("p0", 0, 128, 128)
+        low("p0", 128, 0, 128)
+        cmpq(640, 30, 49)
+        mets("pG", 18, 41, False)
+        for j in range(OS[r], K - 1):
+            ts(blk("Oj", j), R("tau0", 0, 112), C1("pC", 128 + j), ALU.is_lt)
+        if last:
+            tt(R(Xn, 896, 1024), R("Xu", 0, 128), R("Gt", 0, 128), ALU.add)
+        tt(R("ex", 20, 61), R("pG", 0, 41), R("thr", 20, 61), ALU.is_gt)
+        tt(R("Dd", 20, 61), R("ex", 20, 61), R("pA", 276, 317), ALU.mult)
+        group([(R("pG", 64, 104), W("IU"), R("Dd", 20, 60)), (R("pG", 64, 104), W("Ih"), R("ORD", 64, 104)),
+               (R("pG", 64, 104), W("W2"), R("Dd", 21, 61))])
+        cp(R("LP", 16, 56), R("pG", 64, 104))
+        gat(Nn, 128, Nw, "UL", 0, 8)
+        gat(Nn, 1792, Nw, "LP", 0, 8)
+        send("N", r)
+        gat("Xu", 256, Xw, "UL", 8, 48)
+        act(R(Xn, 128, 256), R("p0", 0, 128), AF.Copy)
+        act(R(Xn, 1792, 1920), R("p0", 128, 256), AF.Copy)
+        send("X", r)
+        row = 15 - r
+        AI, SI = "AI%d" % r, "SI%d" % r
+        if last:
+            low("p1", 0, 128, 128)
+        it = [(R("pA", 128, 240), W("Ib"), blk("Oj", j)) for j in range(K - 1)]
+        if last:
+            it.append((R("pA", 128, 240), W("Ib"), R("one", 0, 112)))
+        if prev:
+            it += [(R("pA", 128, 240), RS("Z", 0), R(AI, 0, 112)), (R("pA", 128, 144), RS("Z", 1), R(AI, 112, 128))]
+        if nxt:
+            it += [(R("pA", 224, 240), RS("Z", 14), R(AI, 128, 144)), (R("pA", 128, 240), RS("Z", 15), R(AI, 144, 256))]
+        group(it)
+        tt(R("Dx", 256, M), IND(Xw, R("LP", 16, 56)), R("Xu", 256, M), ALU.subtract)
+        ts(R("Sg", 256, M), R("Dx", 256, M), 1.0, ALU.min, -1.0, ALU.max)
+        ts(R("Gt", 256, M), R("Dx", 256, M), 0.0, ALU.is_gt)
+        if r == 0:
+            cp(R("H0", 128 + HS, 1920), R("Hi", HS, V))
+
+        def wl(i, only_low):
+            return RS("Z", 8 + i) if only_low else RS("Z2", i)
+
+        def wu(i, only_up):
+            return RS("Zn", i) if only_up else RS("Z2", i)
+
+        it = [(R("pA", 0, 112), wl(0, prev), R("Sg", 128, 240)), (R("pA", 0, 16), wl(1, prev), R("Sg", 240, 256)),
+              (R("pA", 96, 112), wu(6, nxt), R("Sg", 0, 16)), (R("pA", 0, 112), wu(7, nxt), R("Sg", 16, 128)),
+              (R("pA", 16, 112), RS("Z2", 1), R("Sg", 256, 352))]
+        it += [(R("pA", 0, 112), RS("Z2", i), R("Sg", 128 + 112 * i, 240 + 112 * i)) for i in range(2, 6)]
+        it += [(R("pA", 0, 96), RS("Z2", 6), R("Sg", 800, M))]
+        group(it, stop=False)
+        if last:
+            low("p1", 128, 256, 320)
+            low("p2", 0, 576, 320)
+        else:
+            up("p1", 0, 256, 512)
+        it = []
+        if prev:
+            it += [(R("pA", 0, 112), RS("Z", 0), R(SI, 0, 112)), (R("pA", 0, 16), RS("Z", 1), R(SI, 112, 128))]
+        if nxt:
+            it += [(R("pA", 96, 112), RS("Zn", 14), R(SI, 128, 144)), (R("pA", 0, 112), RS("Zn", 15), R(SI, 144, 256))]
+        group(it, start=False)
+        if last:
+            tt(R(Xn, 256, 896), R("Xu", 256, M), R("Gt", 256, M), ALU.add)
+            dma("y", EXT(T.yx[:, 128:896]), R(Xn, 256, 1024), "o4")
+            gat(Nn, 256, Nw, "UL", 8, 56)
+            gat(Nn, 1024, Nw, "LP", 8, 56)
+            dma("s", EXT(T.yn[:, 128:1664]), R(Nn, 256, 1792, row=0), "o1")
+            act(R(Xn, 1024, 1472), R("p1", 0, 448), AF.Copy)
+            dma("s", EXT(T.yx[:, 896:1344]), R(Xn, 1024, 1472), "o6")
+            cp(R(Xn, 1472, 1792), R("p2", 0, 320))
+            dma("y", EXT(T.yx[:, 1344:1664]), R(Xn, 1472, 1792), "o7")
+        ts(R("cl", 0, 112), R("pA", 0, 112), 1.0, ALU.min, -1.0, ALU.max)
+        if not last:
+            tt(R("sp", 0, 112), R("cl", 0, 112), R("pA", 128, 240), ALU.add)
+            gat(Nn, 128 + 768, Nw, "UL", 48, 56)
+            gat(Nn, 128 + 896, Nw, "LP", 8, 16)
+            if r == 0:
+                gat(Nn, 256, Nw, "UL", 8, 48)
+                gat(Nn, 1152, Nw, "LP", 16, 56)
+            gat(Hn, 128, Hw, "UL", 0, 8)
+            gat(Hn, 1792, Hw, "LP", 0, 8)
+            dma("y", R(Hn, 128, 256, row=row), R(Nn, 1024, 1152, row=0), "ie%d" % r)
+            dma("y", R(Hn, 1792, 1920, row=row), R(Nn, 896, 1024, row=0), "ie%d" % r)
+            send("H", r)
+            zero(r + 1)
+            if r > 0:
+                gat(Nn, 256, Nw, "UL", 8, 48)
+                gat(Nn, 1152, Nw, "LP", 16, 56)
+            gat(Hn, 256, Hw, "UL", 8, 56)
+            gat(Hn, 1024, Hw, "LP", 8, 56)
+            dma("y", R(Hn, 256, 1024, row=row), R(Nn, 1152, 1920, row=0), "im%d" % r)
+            dma("y", R(Hn, 1024, 1792, row=row), R(Nn, 128, 896, row=0), "im%d" % r)
+            if r > 0:
+                act(R(Xn, 256, 768), R("p1", 0, 512), AF.Copy)
+        else:
+            tt(R("so", 0, 112), R("cl", 0, 112), R("pA", 128, 240), ALU.add)
+            a, b = (0 if prev else 128), (1920 if nxt else 1792)
+            dma("s", EXT(T.yn[:, 0:128]), R(Nn, a, a + E, row=0), "o2")
+            dma("s", EXT(T.yn[:, 1664:V]), R(Nn, b, b + E, row=0), "o2")
+            dma("y", EXT(T.ys[:]), R("so", 0, 112), "o3")
+            dma("s", EXT(T.yx[:, 0:128]), R(Xn, a, a + E), "o5")
+            dma("s", EXT(T.yx[:, 1664:V]), R(Xn, b, b + E), "o5")
+
+    emit(g, T, ops)
+
+
+def emit(g, T, ops):
+    eng = {"v": g.vector, "s": g.scalar, "t": g.tensor, "g": g, "y": g.sync}
+    total, hist = {}, {}
+    for o in ops:
+        if o["sem"]:
+            total[o["sem"]] = total.get(o["sem"], 0) + o["inc"]
+    known = {q: {} for q in eng}
+    for n, o in enumerate(ops):
+        deps = set()
+        acc = [(x, False) for x in o["rd"]] + [(x, True) for x in o["wr"]]
+        for (name, a, b), w in acc:
+            ps = name in PSUM
+            for (m, a2, b2, w2) in hist.get(name, []):
+                p = ops[m]
+                if p["sem"] and p["sem"] == o["sem"]:
+                    continue
+                if ps:
+                    if p["q"] != o["q"]:
+                        deps.add(m)
+                elif (w or w2) and a < b2 and a2 < b:
+                    deps.add(m)
+        for (name, a, b), w in acc:
+            hist.setdefault(name, []).append((n, a, b, w))
+        o["waits"] = []
+        if o["q"] == "x":
+            o["clock"] = {o["sem"]: 1}
+            continue
+        kn = known[o["q"]]
+        for m in sorted(deps, reverse=True):
+            p = ops[m]
+            if p["sem"]:
+                if p["sem"] in kn:
+                    continue
+            elif kn.get(p["q"], -1) >= m:
+                continue
+            o["waits"].append(m)
+            p["mark"] = True
+            for k, x in p["clock"].items():
+                kn[k] = max(kn.get(k, -1), x)
+        o["clock"] = dict(kn)
+        if o["sem"]:
+            o["clock"][o["sem"]] = 1
+        else:
+            o["clock"][o["q"]] = n
+    count = {q: 0 for q in eng}
+    for o in ops:
+        q = o["q"]
+        if q == "x":
+            continue
+        for m in o["waits"]:
+            p = ops[m]
+            if p["sem"]:
+                eng[q].wait_ge(T.sem[p["sem"]], total[p["sem"]])
+            else:
+                eng[q].wait_ge(T.sem["q" + p["q"]], p["num"])
+        ins = o["fn"]()
+        if o["sem"]:
+            if not o.get("own"):
+                ins.then_inc(T.sem[o["sem"]], 16)
+        elif o.get("mark"):
+            count[q] += 1
+            o["num"] = count[q]
+            ins.then_inc(T.sem["q" + q], 1)
+    late = [s for s in total if s[0] == "o"]
+    for s, n in total.items():
+        if s not in late:
+            g.wait_ge(T.sem[s], n)
+    for q in "tgsv":
+        if count[q]:
+            g.wait_ge(T.sem["q" + q], count[q])
+    for s in late:
+        g.wait_ge(T.sem[s], total[s])

@@ -13,49 +13,44 @@ def _sb(name, cols, dt):
 for _r in range(4):
     _sb("X%d" % _r, 2048, B)
     _sb("N%d" % _r, 2048, F)
-for _r in range(3):
     _sb("H%d" % _r, 2048, F)
+for _r in range(3):
     _sb("WV%d" % _r, V, F)
     _sb("WS%d" % _r, V, F)
     _sb("SI%d" % _r, 256, B)
     _sb("AI%d" % _r, 256, B)
 for _n, _c, _d in [
-        ("Hi", V, I), ("P0", V, F), ("P1", V, F), ("sci", 112, I), ("nmi", 112, I), ("nmf", 112, F),
-        ("zer", 112, F), ("zr2", 112, F), ("one", 112, B), ("m256", 8, B), ("cA", 32, B), ("cB", 8, B),
-        ("J", 144, F), ("D0", 128, F), ("pc", 8, I), ("pa", 8, I), ("col", 16, F), ("ta", 144, F),
+        ("Hi", V, I), ("P0", V, F), ("P1", V, F), ("sci", 112, I), ("nmi", 112, I), ("nr", 112, F), ("dg", 336, B), ("NR", V, B),
+        ("zer", 112, F), ("zr2", 112, F), ("one", 112, B), ("m256", 8, B), ("cA", 32, B),
+        ("J", 144, B), ("D0", 128, B), ("pc", 8, I), ("pa", 8, I), ("col", 24, F), ("ta", 144, F),
         ("le", 16, F), ("ge", 16, F),
-        ("ON", 128, B), ("Oh", 128, B), ("On", 128, B), ("Om", 128, B), ("oa", 128, B), ("ob", 128, B),
-        ("LT", 128, B), ("UT", 128, B), ("Ib", 128, B), ("In", 128, B), ("Ik", 128, B), ("I28", 128, B),
-        ("Z", 144, B), ("Zn", 144, B), ("Za", 144, B), ("Z2", 144, B), ("Z3", 144, B),
-        ("Ih", 128, H), ("Is", 128, H), ("SH", 128, H), ("W1", 128, H), ("IU", 128, H), ("W2", 128, H),
+        ("ON", 128, B), ("Oh", 128, B), ("On", 128, B), ("Om", 128, B), ("oa", 128, B), ("ob", 128, B), ("Sel", 128, B),
+        ("LT", 128, B), ("UT", 128, B), ("Ib", 128, B), ("In", 128, B), ("Ik", 128, B), ("Iv", 128, B), ("I56", 128, B), ("I112", 128, H),
+        ("Z", 144, B), ("Zn", 144, B), ("Za", 144, B), ("Z2", 144, B), ("Z3", 144, B), ("Zm", 144, B), ("Z3m", 144, B),
+        ("Ih", 128, H), ("I2", 128, H), ("SH", 128, H), ("W1", 128, H), ("IU", 128, H), ("W2", 128, H),
         ("h1", 128, H), ("h2", 128, H),
-        ("tau0", 112, F), ("tau", 112, F), ("taur", 256, F), ("tr", 64, F), ("t2", 64, F), ("th", 64, F),
-        ("Ec", 896, B), ("Cc", 896, B), ("Mc", 896, H), ("Y", 896, H), ("Ys", 896, B), ("q16", 112, H),
-        ("bb", 32, F), ("td", 16, F), ("th2", 8, F),
-        ("fi", 112, I), ("fu", 112, F), ("fw", 112, F), ("OFF", 112, U),
-        ("wv", 112, F), ("ws", 112, F), ("mx", 112, F), ("UL", 112, U), ("ORD", 112, H),
-        ("Pj", 512, H), ("Oj", 896, B), ("A", 256, B), ("zi", 64, I), ("za", 64, I), ("thr", 64, F),
-        ("Nl", 944, F), ("EQ", 944, B), ("ex", 64, H), ("Dd", 64, H), ("LP", 56, U),
+        ("tau0", 112, F), ("tau", 112, F), ("tau2", 112, H), ("taur", 256, F), ("tr", 64, F), ("t16", 64, H),
+        ("Ec", 896, B), ("Cc", 896, B), ("Mc", 896, H), ("Y", 896, H), ("q16", 112, H), ("qb", 112, B), ("Lb", 112, B),
+        ("bb", 32, F), ("td", 16, F), ("OFF", 112, U),
+        ("wv", 112, F), ("ws", 112, F), ("UL", 112, U), ("ORD", 112, H),
+        ("Pj", 512, H), ("Oj", 896, B), ("A", 256, B), ("zi", 64, I), ("za", 64, I), ("dm", 64, H),
+        ("EQ", 928, B), ("Dd", 64, H), ("LP", 56, U),
         ("Xu", M, B), ("Dx", M, B), ("Sg", M, B), ("Gt", M, B), ("cl", 112, B), ("sp", 112, B), ("so", 112, F)]:
     _sb(_n, _c, _d)
-SCRATCH["nd"] = ("dram", [8, V], F)
 PSUM = ["pA", "pB", "pC", "pE", "pG", "p0", "p1", "p2"]
 for _n in PSUM:
     SCRATCH[_n] = ("psum", [128, 512], F)
 
 KINDS = ["A", "S", "X", "N", "H"]
-SEMAPHORES = ["qv", "qs", "qt", "qg", "lsc", "lnm", "lx", "lh", "lnd", "lN", "o1", "o2", "o3", "o4", "o5", "o6", "o7"]
+SEMAPHORES = ["qv", "qs", "qt", "qg", "lsc", "lnm", "lx", "lh", "lnd", "o1", "o2", "o3", "o4", "o5", "o6", "o7"]
 for _r in range(RO):
-    SEMAPHORES += ["wv%d" % _r, "ws%d" % _r, "ie%d" % _r, "im%d" % _r, "lz%d" % _r]
+    SEMAPHORES += ["wv%d" % _r, "ws%d" % _r, "im%d" % _r, "lz%d" % _r]
     for _k in KINDS:
         SEMAPHORES += ["a%s%d" % (_k, _r), "l%s%d" % (_k, _r)]
 
 MAGIC = 12582912.0
-OFFS = 32.0
 BIG = 4096.0
 KV = [56, 56, 56]
-OS = [0, 2, 3]
-HS = 768
 
 
 def pieces(kind, r):
@@ -123,10 +118,12 @@ def rank_program(g, core, T, topo):
     rel = relays(T, topo, rank)
     ops = []
 
-    def R(name, a, b, step=None, row=None):
+    def R(name, a, b, step=None, row=None, part=None):
         t = T[name]
         if row is not None:
             ap = t[row:128:16, a:b]
+        elif part is not None:
+            ap = t[part[0]:part[1], a:b]
         elif step is not None:
             ap = t[:, a:b:step]
         else:
@@ -166,6 +163,10 @@ def rank_program(g, core, T, topo):
 
     def cp(out, a):
         add("v", lambda: g.vector.tensor_copy(out[0], a[0]), [out], [a])
+
+    def scan(a, b, first):
+        x, o = R("Ec", a, b), R("Cc", a, b)
+        add("v", lambda: g.vector.tensor_tensor_scan(o[0], x[0], x[0], val(first), ALU.add, ALU.max), [o], [x, first])
 
     def act(out, a, func, bias=None, scale=None):
         kw = {}
@@ -244,72 +245,89 @@ def rank_program(g, core, T, topo):
     dma("y", R("Hi", 0, V), EXT(T.hi[:]), "lh")
     iota(R("pc", 0, 1), [[1, 1]], 0, 1, True)
     iota(R("J", 0, 144), [[1, 144]], 0, 0)
-    iota(W("D0"), [[1, 128]], 0, -1)
-    iota(R("cB", 0, 8), [[0, 8]], 56, 0)
-    iota(R("m256", 0, 8), [[0, 8]], -int(BIG) // 16, 0)
-    iota(R("tr", 0, 10), [[16, 10]], 16 * 46, 1)
-    iota(R("tr", 10, 20), [[16, 10]], 0, 1)
+    iota(R("P0", 0, V), [[1, 112], [112, 16]], 0, 0)
+    act(R("zr2", 0, 112), R("zer", 0, 112), AF.Silu)
+    fill(R("m256", 0, 8), -BIG / 16)
     ts(R("pa", 0, 1), R("pc", 0, 1), 112, ALU.bitwise_and)
+    ts(R("pa", 1, 2), R("pc", 0, 1), 7, ALU.bitwise_and)
+    cp(C1("col", 16), R("pc", 0, 1))
     fill(R("cA", 0, 8), -1.0 / 64)
     cp(C1("col", 0), R("pa", 0, 1))
+    ts(C1("col", 17), R("pa", 1, 2), -16.0, ALU.mult, -7.5, ALU.add)
     fill(R("cA", 8, 16), 1.0 / 64)
+    fill(R("cA", 16, 32), -1.0 / 64)
+    ts(W("D0"), W("J"), C1("col", 16), ALU.subtract)
     ts(W("oa"), W("J"), C1("col", 0), ALU.subtract, 0.0, ALU.is_ge)
     ts(W("ob"), W("J"), C1("col", 0), ALU.subtract, 16.0, ALU.is_lt)
-    fill(R("cA", 16, 32), -1.0 / 64)
-    tt(W("ON"), W("oa"), W("ob"), ALU.mult)
     ts(W("Ib"), W("D0"), 0.0, ALU.is_equal)
-    sel("LT", "ON", ALU.is_gt, 0.0, 0)
-    sel("UT", "ON", ALU.is_gt, 0.0, 0, -1)
-    iota(R("tr", 20, 61), [[16, 41]], 16 * 8, 1)
-    iota(R("P0", 0, V), [[1, 112], [112, 16]], int(OFFS), 0)
-    act(R("zr2", 0, 112), R("J", 0, 112), AF.Silu, scale=0.0)
+    ts(W("LT"), W("D0"), 0.0, ALU.is_gt)
+    ts(W("UT"), W("D0"), 0.0, ALU.is_lt)
+    tt(W("ON"), W("oa"), W("ob"), ALU.mult)
     ts(W("Ik"), W("D0"), 0.0, ALU.is_equal, BIG, ALU.mult)
+    tt(W("LT"), W("LT"), W("ob"), ALU.mult)
+    tt(W("UT"), W("UT"), W("oa"), ALU.mult)
     ts(W("Ih"), W("D0"), 0.0, ALU.is_equal)
-    ts(W("Is"), W("D0"), 0.0, ALU.is_equal, 0.0625, ALU.mult)
-    cp(R("nmf", 0, 112), R("nmi", 0, 112))
-    ND = (T.nd[:], [("nd", 0, V)], [])
+    ts(W("I2"), W("D0"), 0.0, ALU.is_equal, 2.0, ALU.mult)
+    ts(W("I112"), W("D0"), 0.0, ALU.is_equal, 112.0, ALU.mult)
+    tt(C1("col", 1), R("pc", 0, 1), R("pa", 0, 1), ALU.subtract)
     lin(W("Oh"), W("ON"), 0.5, 0.0)
     lin(W("On"), W("ON"), -0.5, 0.0)
-    dma("s", ND, R("nmf", 0, 112), "lnd")
-    for j, sc_, bi_ in ((2, -1.0, -15.0), (3, -1.0, -23.0), (4, -1.0, -15.5), (5, 2.0, -1.0), (6, -1.0, 0.0), (7, -112.0, -895.75)):
+    ts(R("le", 0, 16), R("J", 0, 16), C1("col", 1), ALU.is_ge, BIG, ALU.mult)
+    act(R("ta", 0, 128), W("J"), AF.Abs, bias=C1("col", 17))
+    act(W("Sel"), R("ta", 0, 128), AF.Sign, bias=8.0, scale=-1.0)
+    for j, sc_, bi_ in ((2, -1.0, -15.0), (3, -1.0, -23.0), (4, -1.0, -15.5), (7, -112.0, -895.75)):
         lin(C1("col", j), C1("col", 0), sc_, bi_)
-    for i in range(16):
-        dma("y", R("N0", 128, 1920, row=i), ND, "lN")
-    dma("y", R("X0", 128, 1920), EXT(T.x[:]), "lx")
-    lin(W("I28"), W("Ib"), -28.0, 0.0)
+    act(W("Sel"), W("Sel"), AF.Relu)
     hat("Z", 2, 1.0)
     lin(W("Om"), W("ON"), -1.0, 0.0)
-    lin(R("t2", 0, 61), R("tr", 0, 61), -2.0, C1("col", 5))
-    lin(R("th", 0, 61), R("tr", 0, 61), 1.0, C1("col", 6))
+    lin(W("Iv"), W("Ib"), -1792.0, 0.0)
+    lin(W("I56"), W("Ib"), 56.0, 0.0)
+    iota(R("tau", 0, 112), [[1, 112]], 0, 112)
+    iota(R("tr", 0, 10), [[16, 10]], 16 * 46, 1)
+    iota(R("tr", 10, 58), [[16, 48]], 0, 1)
     iota(R("taur", 0, 128), [[2, 128]], 2 * 768 + 1, 0)
     iota(R("taur", 128, 256), [[2, 128]], 0, 0)
-    iota(R("tau", 0, 112), [[1, 112]], 0, 112)
     sel("h1", "ON", ALU.is_equal, 0.0, -1)
     sel("W1", "ON", ALU.is_equal, 0.0, 15)
     sel("SH", "h1", ALU.not_equal, -1.0, 0)
     sel("h2", "Om", ALU.is_equal, 0.0, 1)
     sel("W2", "Om", ALU.is_equal, 0.0, -15)
     sel("IU", "h2", ALU.not_equal, 1.0, 0)
-    iota(R("one", 0, 112), [[0, 112]], 1, 0)
+    lo1 = 0 if prev else 128
 
-    def places():
-        lo1 = 0 if prev else 128
-        iota(R("P1", 0, V), [[1, 112], [112, 16]], int(OFFS) + 128 - lo1, 0)
-        if prev:
-            iota(R("P1", 0, V, step=16), [[1, 112]], int(OFFS), 0)
-            iota(R("P1", 1, 256, step=16), [[1, 16]], int(OFFS) + 112, 0)
-        if nxt:
-            iota(R("P1", 96 * 16 + 14, V, step=16), [[1, 16]], int(OFFS) + 1664 + 256 - lo1, 0)
-            iota(R("P1", 15, V, step=16), [[1, 112]], int(OFFS) + 1680 + 256 - lo1, 0)
+    def places(half):
+        iota(R("P1", M * half, M * half + M), [[1, 56], [112, 16]], 128 - lo1 + 56 * half, 0)
+        if half and prev:
+            iota(R("P1", 0, V, step=16), [[1, 112]], 0, 0)
+            iota(R("P1", 1, 256, step=16), [[1, 16]], 112, 0)
+        if half and nxt:
+            iota(R("P1", 96 * 16 + 14, V, step=16), [[1, 16]], 1664 + 256 - lo1, 0)
+            iota(R("P1", 15, V, step=16), [[1, 112]], 1680 + 256 - lo1, 0)
+        if half:
+            iota(R("one", 0, 112), [[0, 112]], 1, 0)
 
-    def rows():
-        tt(C1("col", 1), R("pc", 0, 1), R("pa", 0, 1), ALU.subtract)
-        ts(R("le", 0, 16), R("J", 0, 16), C1("col", 1), ALU.is_ge, BIG, ALU.mult)
+    places(0)
+
+    def digits(step):
+        if step == 0:
+            cp(blk("dg", 0), R("nmi", 0, 112))
+        elif step == 1:
+            tt(R("nr", 0, 112), R("nmi", 0, 112), blk("dg", 0), ALU.subtract)
+        elif step == 2:
+            cp(blk("dg", 1), R("nr", 0, 112))
+        else:
+            tt(blk("dg", 2), R("nr", 0, 112), blk("dg", 1), ALU.subtract)
+            for d in range(3):
+                dma("y", R("NR", 0, V, part=(8 * d, 8 * d + 8)), blk("dg", d), "lnd")
+            dma("y", R("X0", 128, 1920), EXT(T.x[:]), "lx")
 
     def consts2():
+        hat("Z3", 4, 1.5)
+        hat("Za", 3, 1.0)
+        lin(R("Zm", 0, 144), R("Z", 0, 144), -2048.0, 0.0)
         lin(R("ge", 1, 16), R("le", 0, 15), -1.0, BIG)
         lin(C1("col", 8), C1("le", 7), 895.5 / BIG, C1("col", 7))
-        lin(W("In"), W("Ib"), -1.0, 0.0)
+        lin(R("Z3m", 0, 144), R("Z3", 0, 144), -2048.0, 0.0)
         for j, (a, b, jl, jg) in enumerate(((0, 16, 1, 15), (16, 96, 0, 15), (96, 112, 0, 14))):
             c_ = C1("col", 8)
             if prev:
@@ -319,6 +337,7 @@ def rank_program(g, core, T, topo):
                 lin(C1("col", 12 + j), C1("ge", jg), 1.0, c_)
                 c_ = C1("col", 12 + j)
             lin(R("tau0", a, b), R("tau", a, b), 1.0, c_)
+        lin(W("In"), W("Ib"), -1.0, 0.0)
         lin(R("Zn", 0, 144), R("Z", 0, 144), -1.0, 0.0)
 
     def up(ps, o, c, n):
@@ -332,152 +351,159 @@ def rank_program(g, core, T, topo):
         act(R(dst, c0, c0 + 16 * (b - a)), IND(win, R(off, a, b)), AF.Copy)
 
     def mets(ps, c0, n, first):
-        it = [(R(ps, 0, n), RS("Z3", i), R("EQ", 16 * c0 + i, 16 * (c0 + n), step=16)) for i in range(15)]
+        it = [(R(ps, 0, n), RS("Z3m", i), R("EQ", 16 * c0 + i, 16 * (c0 + n), step=16)) for i in range(15)]
         if first:
-            it.append((R(ps, 1, n), RS("Z", 0), R("EQ", 15, 16 * (n - 1), step=16)))
+            it.append((R(ps, 1, n), RS("Zm", 0), R("EQ", 15, 16 * (n - 1), step=16)))
         else:
-            it.append((R(ps, 0, n), RS("Z", 0), R("EQ", 16 * c0 - 1, 16 * (c0 + n - 1), step=16)))
-        it.append((R(ps, 0, n), RS("Z", 15), R("EQ", 16 * c0 + 15, 16 * (c0 + n), step=16)))
+            it.append((R(ps, 0, n), RS("Zm", 0), R("EQ", 16 * c0 - 1, 16 * (c0 + n - 1), step=16)))
+        it.append((R(ps, 0, n), RS("Zm", 15), R("EQ", 16 * c0 + 15, 16 * (c0 + n), step=16)))
         group(it)
 
     for r in range(RO):
         K = 4 + 2 * r
+        K2 = K // 2
         last = r == RO - 1
-        lo, hi = (128, 1920) if r == 0 else (0 if prev else 128, 2048 if nxt else 1920)
+        lo, hi = (128, 1920) if r == 0 else (lo1, 2048 if nxt else 1920)
         Xc, Xn, Nn, Hn = "X%d" % r, "X%d" % (r + 1), "N%d" % (r + 1), "H%d" % (r + 1)
         Xw, Nw, Hw = R(Xc, lo, hi), R("N%d" % r, lo, hi), R("H%d" % r, lo, hi)
         PAY = "P0" if r == 0 else "P1"
-        for j in range(K):
-            k = K - 1 - j
-            if r == 0:
-                ts(blk("Ec", j), R("sci", 0, 112), float(k), ALU.is_equal)
-            else:
-                ts(blk("Ec", j), R("sp", 0, 112), float(k - 1), ALU.is_equal)
         Wd = 112 * K
-        for ps, a, b in (("p2", 0, K // 2), ("p0", K // 2, K)):
-            group([(R(ps, 0, 112 * (b - a)), W("Ik"), R("Ec", 112 * a, 112 * b))], stop=False)
-        add("v", lambda Wd=Wd: g.vector.tensor_tensor_scan(T.Cc[:, 0:Wd], T.Ec[:, 0:Wd], T.Ec[:, 0:Wd], 0.0, ALU.add, ALU.max),
-            [R("Cc", 0, Wd)], [R("Ec", 0, Wd)])
+        group([(R("pC", 128, 160), W("ON"), R("cA", 0, 32))], stop=False)
+        for ps, pb, a in (("p2", "pB", 0), ("p0", "pE", K2)):
+            b = a + K2
+            for j in range(a, b):
+                k = K - 1 - j
+                if r == 0:
+                    ts(blk("Ec", j), R("sci", 0, 112), float(k), ALU.is_equal)
+                else:
+                    ts(blk("Ec", j), R("sp", 0, 112), float(k - 1), ALU.is_equal)
+            group([(R(ps, 0, 112 * K2), W("Ik"), R("Ec", 112 * a, 112 * b))], stop=False)
+            scan(112 * a, 112 * b, C1("Cc", 112 * a - 1) if a else 0.0)
+            a1 = max(a, 1)
+            group([(R(pb, 128 + a, 128 + b), W("ON"), R("m256", a, b)),
+                   (R(pb, 128 + a, 128 + b), W("LT"), R("Cc", 112 * a + 111, 112 * b, step=112)),
+                   (R(pb, 128 + a1, 128 + b), W("UT"), R("Cc", 112 * a1 - 1, 112 * (b - 1), step=112))])
+            group([(R(ps, 0, 112 * K2), W("Ib"), R("Cc", 112 * a, 112 * b))], start=False)
         hiK, hiJ = R("Cc", 111, Wd, step=112), R("Cc", 111, Wd - 112, step=112)
-        group([(R("pC", 128, 160), W("ON"), R("cA", 0, 32)), (R("pC", 136, 144), W("ON"), R("cB", 0, 8))], stop=False)
-        group([(R("pB", 0, K), W("ON"), R("m256", 0, K)), (R("pB", 0, K), W("LT"), hiK), (R("pB", 1, K), W("UT"), hiJ)])
-        group([(R("p2", 0, Wd // 2), W("Ib"), R("Cc", 0, Wd // 2))], start=False)
         group([(R("pC", 128, 128 + K), W("Oh"), hiK), (R("pC", 136, 136 + K), W("On"), hiK),
                (R("pC", 145, 144 + K), W("Oh"), hiJ), (R("pC", 153, 152 + K), W("Oh"), hiJ)], start=False)
-        group([(R("p0", 0, Wd // 2), W("Ib"), R("Cc", Wd // 2, Wd))], start=False)
-        for j in range(K // 2):
-            ts(blk("Mc", j), blk("p2", j), C1("pB", j), ALU.add, 0.0, ALU.max)
-        ts(R("bb", 0, 32), R("pC", 128, 160), MAGIC, ALU.add, -MAGIC, ALU.add)
-        for j in range(K // 2, K):
-            ts(blk("Mc", j), blk("p0", j - K // 2), C1("pB", j), ALU.add, 0.0, ALU.max)
-        group([(R("pC", 0, 112), W("Ih"), blk("Mc", j)) for j in range(K)])
-        lin(R("th2", 0, 8), R("bb", 0, 8), -2.0, -0.5)
-        tt(R("td", 0, 16), R("bb", 0, 16), R("bb", 16, 32), ALU.add)
-        cp(R("q16", 0, 112), R("pC", 0, 112))
-        ns = K - 1
-        for j in range(ns):
-            act(blk("Ys", j), R("pC", 0, 112), AF.Sign, bias=C1("th2", j))
         if r == 0:
-            hat("Z3", 4, 1.5)
-            hat("Za", 3, 1.0)
+            digits(0)
+        for j in range(K2):
+            ts(blk("Mc", j), blk("p2", j), C1("pB", 128 + j), ALU.add, 0.0, ALU.max)
+        if r == 0:
+            digits(1)
+        ts(R("bb", 0, 32), R("pC", 128, 160), MAGIC, ALU.add, -MAGIC, ALU.add)
+        for j in range(K2, K):
+            ts(blk("Mc", j), blk("p0", j - K2), C1("pE", 128 + j), ALU.add, 0.0, ALU.max)
+        group([(R("pC", 0, 112), W("Ih"), blk("Mc", j)) for j in range(K)])
+        tt(R("td", 0, 16), R("bb", 0, 16), R("bb", 16, 32), ALU.add)
+        if r == 0:
+            digits(2)
+            consts2()
+        cp(R("q16", 0, 112), R("pC", 0, 112))
+        if r == 0:
+            digits(3)
         for j in range(K):
             ts(blk("Y", j), R("q16", 0, 112), C1("td", j), ALU.is_gt, C1("td", 8 + j), ALU.mult)
-        it = [(W("Is"), R("q16", 0, 112))]
-        for j in range(K):
-            it.append((W("Is"), blk("Y", j)))
-            if j > 0:
-                it.append((W("I28"), blk("Ys", j - 1)))
-        group([(R("pG", 256, 368), a, b) for a, b in it])
+        TT = R("pG", 256, 368)
+        group([(TT, W("I2"), R("q16", 0, 112))] + [(TT, W("I2"), blk("Y", j)) for j in range(K)])
+        ZZ = R("pB", 256, 368)
+        group([(ZZ, W("I112"), R("q16", 0, 112))] + [(ZZ, W("I112"), blk("Y", j)) for j in range(K)], stop=False)
         group([(R("pE", 64, 65), RS("Z", j), C1("Cc", 112 * j + 111)) for j in range(K - 1)])
-        if r > 0:
-            up("p2", 0, 768, 128)
-            up("p2", 128, 0, 128)
-            low("p2", 256, 128, 256)
-            low("p0", 0, 384, 512)
-        else:
-            rows()
-        ts(R("fi", 0, 112), R("pG", 256, 368), -17.0 / 32.0 - 28.0 * ns, ALU.add)
-        ts(R("fu", 0, 112), R("fi", 0, 112), 1791.0 / 1792.0, ALU.mult, 0.0625 + 28.0 * ns, ALU.add)
-        tt(R("fw", 0, 112), R("pG", 256, 368), R("fu", 0, 112), ALU.subtract)
-        ts(R("OFF", 0, 112), R("fw", 0, 112), 1792.0, ALU.mult, 0.25, ALU.add)
+        ts(R("qb", 0, 112), TT, 1.0 / 32, ALU.mult, 136.0 - 17.0 / 32, ALU.add)
+        tt(R("Lb", 0, 112), TT, R("q16", 0, 112), ALU.is_le)
+        group([(ZZ, W("Iv"), R("qb", 0, 112)), (ZZ, W("Ib"), R("qb", 0, 112)), (ZZ, W("I56"), R("Lb", 0, 112))], start=False)
+        ts(R("OFF", 0, 112), ZZ, 1791.0 * 136 - 112 + 0.25, ALU.add)
         kv = KV[r]
         act(IND(R("WS%d" % r, 0, V), R("OFF", kv, 112)), R(PAY, 16 * kv, V), AF.Silu)
         cp(IND(R("WV%d" % r, 0, V), R("OFF", 0, kv)), R(PAY, 0, 16 * kv))
         dma("y", R("wv", 0, 112), R("WV%d" % r, 0, V, row=0), "wv%d" % r)
         dma("s", R("ws", 0, 112), R("WS%d" % r, 0, V, row=0), "ws%d" % r)
         if r == 0:
-            consts2()
+            for j, ps in enumerate(("p1", "p2", "p0", "pB")):
+                group([(R(ps, 0, 448), R("Sel", 0, 128, part=(0, 24)), R("NR", 448 * j, 448 * j + 448, part=(0, 24)))])
+                act(R("N0", 128 + 448 * j, 576 + 448 * j), R(ps, 0, 448), AF.Copy)
         else:
-            if r == 1:
-                act(R(Xc, 256, 768), R("p1", 0, 512), AF.Copy)
+            up("p2", 0, 768, 128)
+            up("p2", 128, 0, 128)
+            low("p2", 256, 128, 256)
+            low("p0", 0, 384, 512)
+            act(R(Xc, 256, 768), R("p1", 0, 512), AF.Copy)
             act(R(Xc, 768, 1280), R("p2", 0, 512), AF.Copy)
             act(R(Xc, 1280, 1792), R("p0", 0, 512), AF.Copy)
         ts(R("A", 0, 256), R("taur", 0, 256), C1("pE", 64), ALU.is_lt)
         send("A", r)
         if r == 0:
-            places()
+            places(1)
+            ts(R("t16", 0, 58), R("tr", 0, 58), C1("col", 0), ALU.subtract)
+            ts(R("tau2", 0, 112), R("tau0", 0, 112), 2.0, ALU.mult, 0.5, ALU.add)
         for j in range(K - 1):
-            ts(R("Pj", 64 * j, 64 * j + 61), R("t2", 0, 61), C1("th2", j), ALU.is_lt, C1("td", 8 + j), ALU.mult)
-        group([(R("pG", 128, 189), W("Ih"), R("Pj", 64 * j, 64 * j + 61)) for j in range(K - 1)])
-        for j in range(OS[r]):
-            ts(blk("Oj", j), R("tau0", 0, 112), C1("pC", 128 + j), ALU.is_lt)
+            ts(R("Pj", 64 * j, 64 * j + 58), R("t16", 0, 58), C1("bb", j), ALU.is_ge, C1("td", 8 + j), ALU.mult)
+        group([(R("pG", 128, 186), W("Ih"), R("Pj", 64 * j, 64 * j + 58)) for j in range(K - 1)]
+              + [(R("pG", 128, 186), W("Ih"), R("t16", 0, 58))])
+        for j in range(K - 1):
+            ts(blk("Oj", j), R("tau2", 0, 112), 0.5, ALU.mult, C1("pC", 128 + j), ALU.is_lt)
         if r == 0:
             tt(R("Z2", 0, 144), R("Za", 0, 144), R("Z", 0, 144), ALU.subtract)
-        tt(R("zi", 0, 61), R("pG", 128, 189), R("th", 0, 61), ALU.add)
-        ts(R("za", 0, 61), R("zi", 0, 61), 1, ALU.bitwise_and)
-        ts(R("thr", 0, 61), R("za", 0, 61), 0.0, ALU.is_equal, 100.0, ALU.mult)
+        cp(R("zi", 0, 58), R("pG", 128, 186))
         if r == 0:
-            cp(R("H0", 128, 128 + HS), R("Hi", 0, HS))
-        tt(R("mx", 0, 112), R("wv", 0, 112), R("ws", 0, 112), ALU.max)
-        ts(R("UL", 0, 112), R("mx", 0, 112), 0.25 - OFFS, ALU.add)
-        ts(R("ORD", 0, 112), R("mx", 0, 112), MAGIC - OFFS, ALU.add, -MAGIC, ALU.add)
-        for (o, a, n) in ((0, 46, 10), (10, 0, 10), (20, 8, 41)):
+            cp(R("H0", 128, 1024), R("Hi", 0, M))
+        ts(R("za", 0, 58), R("zi", 0, 58), 1, ALU.bitwise_and)
+        if r == 0:
+            cp(R("H0", 1024, 1920), R("Hi", M, V))
+        tt(R("ORD", 0, 112), R("wv", 0, 112), R("ws", 0, 112), ALU.max)
+        cp(R("UL", 0, 112), R("ORD", 0, 112))
+        for (o, a, n) in ((0, 46, 10), (10, 0, 48)):
             group([(R("pA", 256 + o, 256 + o + n), W("SH"), R("ORD", 56 + a, 56 + a + n)),
                    (R("pA", 256 + o, 256 + o + n), W("W1"), R("ORD", 55 + a, 55 + a + n))])
 
         def cmpq(c0, a, b):
-            n = 16 * (b - a)
-            tt(R("EQ", c0, c0 + n), IND(Hw if r else R("Hi", 0, V), R("UL", a, b)), R("Nl", c0, c0 + n), ALU.is_equal)
+            tt(R("EQ", c0, c0 + 16 * (b - a)), IND(Nw, R("UL", 56 + a, 56 + b)), R(Hn, 128 + 16 * a, 128 + 16 * b), ALU.is_equal)
 
-        gat("Nl", 0, Nw, "UL", 102, 112)
-        gat("Nl", 160, Nw, "UL", 56, 66)
-        gat("Nl", 320, Nw, "UL", 66, 86)
+        def his(a, b):
+            gat(Hn, 128 + 16 * a, Hw, "UL", a, b)
+
+        his(46, 56)
+        his(0, 10)
+        tt(R("dm", 0, 58), R("pA", 256, 314), R("za", 0, 58), ALU.mult)
+        his(10, 28)
+        his(28, 46)
         gat("Xu", 0, Xw, "UL", 48, 56)
         gat("Xu", 128, Xw, "UL", 0, 8)
-        gat("Nl", 640, Nw, "UL", 86, 105)
+        gat("Xu", 256, Xw, "UL", 8, 48)
         cmpq(0, 46, 56)
         cmpq(160, 0, 10)
         mets("pE", 0, 20, True)
-        cmpq(320, 10, 30)
-        tt(R("ex", 0, 20), R("pE", 0, 20), R("thr", 0, 20), ALU.is_gt)
-        tt(R("Dd", 0, 20), R("ex", 0, 20), R("pA", 256, 276), ALU.mult)
+        cmpq(320, 10, 28)
+        tt(R("Dd", 0, 20), R("pE", 0, 20), R("dm", 0, 20), ALU.max)
         group([(R("pE", 32, 48), W("IU"), R("Dd", 2, 18)), (R("pE", 32, 40), W("Ih"), R("ORD", 104, 112)),
                (R("pE", 40, 48), W("Ih"), R("ORD", 56, 64)), (R("pE", 32, 48), W("W2"), R("Dd", 3, 19))])
+        cmpq(608, 28, 48)
+        mets("pG", 20, 38, False)
         cp(R("LP", 0, 16), R("pE", 32, 48))
         tt(R("Dx", 0, 256), IND(Xw, R("LP", 0, 16)), R("Xu", 0, 256), ALU.subtract)
         ts(R("Sg", 0, 256), R("Dx", 0, 256), 1.0, ALU.min, -1.0, ALU.max)
         send("S", r)
+        if last:
+            gat(Nn, 128, Nw, "UL", 0, 8)
+            gat(Nn, 1792, Nw, "LP", 0, 8)
+        tt(R("Dd", 20, 58), R("pG", 0, 38), R("dm", 20, 58), ALU.max)
+        group([(R("pG", 64, 104), W("IU"), R("Dd", 18, 58)), (R("pG", 64, 104), W("Ih"), R("ORD", 64, 104)),
+               (R("pG", 64, 103), W("W2"), R("Dd", 19, 58)), (R("pG", 103, 104), W("W2"), R("Dd", 2, 3))])
         ts(R("Gt", 0, 256), R("Dx", 0, 256), 0.0, ALU.is_gt)
         up("p0", 0, 128, 128)
         low("p0", 128, 0, 128)
-        cmpq(640, 30, 49)
-        mets("pG", 18, 41, False)
-        for j in range(OS[r], K - 1):
-            ts(blk("Oj", j), R("tau0", 0, 112), C1("pC", 128 + j), ALU.is_lt)
+        cp(R("LP", 16, 56), R("pG", 64, 104))
         if last:
             tt(R(Xn, 896, 1024), R("Xu", 0, 128), R("Gt", 0, 128), ALU.add)
-        tt(R("ex", 20, 61), R("pG", 0, 41), R("thr", 20, 61), ALU.is_gt)
-        tt(R("Dd", 20, 61), R("ex", 20, 61), R("pA", 276, 317), ALU.mult)
-        group([(R("pG", 64, 104), W("IU"), R("Dd", 20, 60)), (R("pG", 64, 104), W("Ih"), R("ORD", 64, 104)),
-               (R("pG", 64, 104), W("W2"), R("Dd", 21, 61))])
-        cp(R("LP", 16, 56), R("pG", 64, 104))
-        gat(Nn, 128, Nw, "UL", 0, 8)
-        gat(Nn, 1792, Nw, "LP", 0, 8)
-        send("N", r)
-        gat("Xu", 256, Xw, "UL", 8, 48)
+        else:
+            gat(Nn, 128, Nw, "UL", 0, 56)
         act(R(Xn, 128, 256), R("p0", 0, 128), AF.Copy)
         act(R(Xn, 1792, 1920), R("p0", 128, 256), AF.Copy)
         send("X", r)
+        if last:
+            send("N", r)
         row = 15 - r
         AI, SI = "AI%d" % r, "SI%d" % r
         if last:
@@ -493,8 +519,6 @@ def rank_program(g, core, T, topo):
         tt(R("Dx", 256, M), IND(Xw, R("LP", 16, 56)), R("Xu", 256, M), ALU.subtract)
         ts(R("Sg", 256, M), R("Dx", 256, M), 1.0, ALU.min, -1.0, ALU.max)
         ts(R("Gt", 256, M), R("Dx", 256, M), 0.0, ALU.is_gt)
-        if r == 0:
-            cp(R("H0", 128 + HS, 1920), R("Hi", HS, V))
 
         def wl(i, only_low):
             return RS("Z", 8 + i) if only_low else RS("Z2", i)
@@ -532,26 +556,15 @@ def rank_program(g, core, T, topo):
         ts(R("cl", 0, 112), R("pA", 0, 112), 1.0, ALU.min, -1.0, ALU.max)
         if not last:
             tt(R("sp", 0, 112), R("cl", 0, 112), R("pA", 128, 240), ALU.add)
-            gat(Nn, 128 + 768, Nw, "UL", 48, 56)
-            gat(Nn, 128 + 896, Nw, "LP", 8, 16)
-            if r == 0:
-                gat(Nn, 256, Nw, "UL", 8, 48)
-                gat(Nn, 1152, Nw, "LP", 16, 56)
-            gat(Hn, 128, Hw, "UL", 0, 8)
+            gat(Nn, 1792, Nw, "LP", 0, 8)
+            send("N", r)
+            gat(Nn, 1024, Nw, "LP", 8, 56)
             gat(Hn, 1792, Hw, "LP", 0, 8)
-            dma("y", R(Hn, 128, 256, row=row), R(Nn, 1024, 1152, row=0), "ie%d" % r)
-            dma("y", R(Hn, 1792, 1920, row=row), R(Nn, 896, 1024, row=0), "ie%d" % r)
+            gat(Hn, 1024, Hw, "LP", 8, 56)
+            dma("y", R(Hn, 128, 1024, row=row), R(Nn, 1024, 1920, row=0), "im%d" % r)
+            dma("y", R(Hn, 1024, 1920, row=row), R(Nn, 128, 1024, row=0), "im%d" % r)
             send("H", r)
             zero(r + 1)
-            if r > 0:
-                gat(Nn, 256, Nw, "UL", 8, 48)
-                gat(Nn, 1152, Nw, "LP", 16, 56)
-            gat(Hn, 256, Hw, "UL", 8, 56)
-            gat(Hn, 1024, Hw, "LP", 8, 56)
-            dma("y", R(Hn, 256, 1024, row=row), R(Nn, 1152, 1920, row=0), "im%d" % r)
-            dma("y", R(Hn, 1024, 1792, row=row), R(Nn, 128, 896, row=0), "im%d" % r)
-            if r > 0:
-                act(R(Xn, 256, 768), R("p1", 0, 512), AF.Copy)
         else:
             tt(R("so", 0, 112), R("cl", 0, 112), R("pA", 128, 240), ALU.add)
             a, b = (0 if prev else 128), (1920 if nxt else 1792)

@@ -3,6 +3,7 @@ from concourse.mybir import AluOpType as ALU, ActivationFunctionType as AF
 
 V, M, E, RO = 1792, 896, 128, 3
 F, B, H, I, U = "float32", "bfloat16", "float16", "int32", "uint16"
+KV = [50, 56, 56]
 SCRATCH = {}
 
 
@@ -15,12 +16,11 @@ for _r in range(4):
     _sb("N%d" % _r, 2048, F)
     _sb("H%d" % _r, 2048, F)
 for _r in range(3):
-    _sb("WV%d" % _r, V, F)
     _sb("WS%d" % _r, V, F)
     _sb("SI%d" % _r, 256, B)
     _sb("AI%d" % _r, 256, B)
 for _n, _c, _d in [
-        ("Hi", V, I), ("P0", V, F), ("P1", V, F), ("sci", 112, I), ("nmi", 112, I), ("nr", 112, F), ("dg", 336, B), ("NR", V, B),
+        ("WV", V, F), ("Hi", V, I), ("P0", V, F), ("P1", V, F), ("sci", 112, I), ("nmi", 112, I), ("nr", 112, F), ("dg", 336, B), ("NR", V, B),
         ("zer", 112, F), ("zr2", 112, F), ("one", 112, B), ("m256", 8, B), ("cA", 32, B),
         ("J", 144, B), ("D0", 128, B), ("pc", 8, I), ("pa", 8, I), ("col", 24, F), ("ta", 144, F),
         ("le", 16, F), ("ge", 16, F),
@@ -42,7 +42,7 @@ for _n in PSUM:
     SCRATCH[_n] = ("psum", [128, 512], F)
 
 KINDS = ["A", "S", "X", "N", "H"]
-SEMAPHORES = ["qv", "qs", "qt", "qg", "lsc", "lnm", "lx", "lh", "lnd", "o1", "o2", "o3", "o4", "o5", "o6", "o7"]
+SEMAPHORES = ["qv", "qs", "qt", "qg", "lsc", "lnm", "lx", "lh", "lnd", "o1", "o2", "o3", "o4", "o5", "o6", "o7", "o8"]
 for _r in range(RO):
     SEMAPHORES += ["wv%d" % _r, "ws%d" % _r, "im%d" % _r, "lz%d" % _r]
     for _k in KINDS:
@@ -50,7 +50,6 @@ for _r in range(RO):
 
 MAGIC = 12582912.0
 BIG = 4096.0
-KV = [56, 56, 56]
 
 
 def pieces(kind, r):
@@ -228,7 +227,7 @@ def rank_program(g, core, T, topo):
         return R(name, 112 * j, 112 * j + 112)
 
     def zero(r):
-        dma("y", R("WV%d" % r, 0, V, row=0), R("zr2" if r else "zer", 0, 112), "lz%d" % r)
+        dma("y", R("WV", 0, V, row=0), R("zer", 0, 112), "lz%d" % r)
         dma("y", R("WS%d" % r, 0, V, row=0), R("zr2" if r else "zer", 0, 112), "lz%d" % r)
 
     def sel(out, a, op, c, base, sign=1):
@@ -245,6 +244,9 @@ def rank_program(g, core, T, topo):
     dma("y", R("Hi", 0, V), EXT(T.hi[:]), "lh")
     iota(R("pc", 0, 1), [[1, 1]], 0, 1, True)
     iota(R("J", 0, 144), [[1, 144]], 0, 0)
+    iota(R("tau", 0, 112), [[1, 112]], 0, 112)
+    iota(R("tr", 0, 10), [[16, 10]], 16 * 46, 1)
+    iota(R("tr", 10, 58), [[16, 48]], 0, 1)
     iota(R("P0", 0, V), [[1, 112], [112, 16]], 0, 0)
     act(R("zr2", 0, 112), R("zer", 0, 112), AF.Silu)
     fill(R("m256", 0, 8), -BIG / 16)
@@ -266,13 +268,9 @@ def rank_program(g, core, T, topo):
     ts(W("Ik"), W("D0"), 0.0, ALU.is_equal, BIG, ALU.mult)
     tt(W("LT"), W("LT"), W("ob"), ALU.mult)
     tt(W("UT"), W("UT"), W("oa"), ALU.mult)
-    ts(W("Ih"), W("D0"), 0.0, ALU.is_equal)
-    ts(W("I2"), W("D0"), 0.0, ALU.is_equal, 2.0, ALU.mult)
-    ts(W("I112"), W("D0"), 0.0, ALU.is_equal, 112.0, ALU.mult)
     tt(C1("col", 1), R("pc", 0, 1), R("pa", 0, 1), ALU.subtract)
     lin(W("Oh"), W("ON"), 0.5, 0.0)
     lin(W("On"), W("ON"), -0.5, 0.0)
-    ts(R("le", 0, 16), R("J", 0, 16), C1("col", 1), ALU.is_ge, BIG, ALU.mult)
     act(R("ta", 0, 128), W("J"), AF.Abs, bias=C1("col", 17))
     act(W("Sel"), R("ta", 0, 128), AF.Sign, bias=8.0, scale=-1.0)
     for j, sc_, bi_ in ((2, -1.0, -15.0), (3, -1.0, -23.0), (4, -1.0, -15.5), (7, -112.0, -895.75)):
@@ -282,9 +280,6 @@ def rank_program(g, core, T, topo):
     lin(W("Om"), W("ON"), -1.0, 0.0)
     lin(W("Iv"), W("Ib"), -1792.0, 0.0)
     lin(W("I56"), W("Ib"), 56.0, 0.0)
-    iota(R("tau", 0, 112), [[1, 112]], 0, 112)
-    iota(R("tr", 0, 10), [[16, 10]], 16 * 46, 1)
-    iota(R("tr", 10, 58), [[16, 48]], 0, 1)
     iota(R("taur", 0, 128), [[2, 128]], 2 * 768 + 1, 0)
     iota(R("taur", 128, 256), [[2, 128]], 0, 0)
     sel("h1", "ON", ALU.is_equal, 0.0, -1)
@@ -322,23 +317,21 @@ def rank_program(g, core, T, topo):
             dma("y", R("X0", 128, 1920), EXT(T.x[:]), "lx")
 
     def consts2():
-        hat("Z3", 4, 1.5)
-        hat("Za", 3, 1.0)
-        lin(R("Zm", 0, 144), R("Z", 0, 144), -2048.0, 0.0)
         lin(R("ge", 1, 16), R("le", 0, 15), -1.0, BIG)
         lin(C1("col", 8), C1("le", 7), 895.5 / BIG, C1("col", 7))
+        hat("Z3", 4, 1.5)
+        parts = ((0, 16, 1, 15), (16, 96, 0, 15), (96, 112, 0, 14))
+        cs = [8, 8, 8]
+        for on, name, k, c0 in ((prev, "le", 2, 9), (nxt, "ge", 3, 12)):
+            for j, p in enumerate(parts if on else ()):
+                lin(C1("col", c0 + j), C1(name, p[k]), 1.0, C1("col", cs[j]))
+                cs[j] = c0 + j
+            lin(R("Zm" if k == 2 else "Zn", 0, 144), R("Z", 0, 144), -2048.0 if k == 2 else -1.0, 0.0)
+        hat("Za", 3, 1.0)
+        for j, p in enumerate(parts):
+            lin(R("tau0", p[0], p[1]), R("tau", p[0], p[1]), 1.0, C1("col", cs[j]))
         lin(R("Z3m", 0, 144), R("Z3", 0, 144), -2048.0, 0.0)
-        for j, (a, b, jl, jg) in enumerate(((0, 16, 1, 15), (16, 96, 0, 15), (96, 112, 0, 14))):
-            c_ = C1("col", 8)
-            if prev:
-                lin(C1("col", 9 + j), C1("le", jl), 1.0, c_)
-                c_ = C1("col", 9 + j)
-            if nxt:
-                lin(C1("col", 12 + j), C1("ge", jg), 1.0, c_)
-                c_ = C1("col", 12 + j)
-            lin(R("tau0", a, b), R("tau", a, b), 1.0, c_)
         lin(W("In"), W("Ib"), -1.0, 0.0)
-        lin(R("Zn", 0, 144), R("Z", 0, 144), -1.0, 0.0)
 
     def up(ps, o, c, n):
         group([(R(ps, o, o + n), W("Ib"), R("Xu", c, c + n)), (R(ps, o, o + n), W("Ib"), R("Gt", c, c + n))])
@@ -371,12 +364,14 @@ def rank_program(g, core, T, topo):
         group([(R("pC", 128, 160), W("ON"), R("cA", 0, 32))], stop=False)
         for ps, pb, a in (("p2", "pB", 0), ("p0", "pE", K2)):
             b = a + K2
-            for j in range(a, b):
+            for j in range(a + 1 if a else 0, min(b + 1, K)):
                 k = K - 1 - j
                 if r == 0:
                     ts(blk("Ec", j), R("sci", 0, 112), float(k), ALU.is_equal)
                 else:
                     ts(blk("Ec", j), R("sp", 0, 112), float(k - 1), ALU.is_equal)
+            if r == 0 and a:
+                digits(0)
             group([(R(ps, 0, 112 * K2), W("Ik"), R("Ec", 112 * a, 112 * b))], stop=False)
             scan(112 * a, 112 * b, C1("Cc", 112 * a - 1) if a else 0.0)
             a1 = max(a, 1)
@@ -388,37 +383,44 @@ def rank_program(g, core, T, topo):
         group([(R("pC", 128, 128 + K), W("Oh"), hiK), (R("pC", 136, 136 + K), W("On"), hiK),
                (R("pC", 145, 144 + K), W("Oh"), hiJ), (R("pC", 153, 152 + K), W("Oh"), hiJ)], start=False)
         if r == 0:
-            digits(0)
+            ts(W("Ih"), W("D0"), 0.0, ALU.is_equal)
+            ts(R("le", 0, 16), R("J", 0, 16), C1("col", 1), ALU.is_ge, BIG, ALU.mult)
+            consts2()
         for j in range(K2):
             ts(blk("Mc", j), blk("p2", j), C1("pB", 128 + j), ALU.add, 0.0, ALU.max)
         if r == 0:
             digits(1)
-        ts(R("bb", 0, 32), R("pC", 128, 160), MAGIC, ALU.add, -MAGIC, ALU.add)
         for j in range(K2, K):
+            if j == K - 1:
+                ts(R("bb", 0, 32), R("pC", 128, 160), MAGIC, ALU.add, -MAGIC, ALU.add)
             ts(blk("Mc", j), blk("p0", j - K2), C1("pE", 128 + j), ALU.add, 0.0, ALU.max)
-        group([(R("pC", 0, 112), W("Ih"), blk("Mc", j)) for j in range(K)])
+        group([(R("pA", 384, 496), W("Ih"), blk("Mc", j)) for j in range(K)])
         tt(R("td", 0, 16), R("bb", 0, 16), R("bb", 16, 32), ALU.add)
         if r == 0:
             digits(2)
-            consts2()
-        cp(R("q16", 0, 112), R("pC", 0, 112))
+            ts(W("I2"), W("D0"), 0.0, ALU.is_equal, 2.0, ALU.mult)
+            ts(W("I112"), W("D0"), 0.0, ALU.is_equal, 112.0, ALU.mult)
+        cp(R("q16", 0, 112), R("pA", 384, 496))
         if r == 0:
-            digits(3)
+            ts(R("t16", 0, 58), R("tr", 0, 58), C1("col", 0), ALU.subtract)
         for j in range(K):
             ts(blk("Y", j), R("q16", 0, 112), C1("td", j), ALU.is_gt, C1("td", 8 + j), ALU.mult)
         TT = R("pG", 256, 368)
-        group([(TT, W("I2"), R("q16", 0, 112))] + [(TT, W("I2"), blk("Y", j)) for j in range(K)])
         ZZ = R("pB", 256, 368)
-        group([(ZZ, W("I112"), R("q16", 0, 112))] + [(ZZ, W("I112"), blk("Y", j)) for j in range(K)], stop=False)
-        group([(R("pE", 64, 65), RS("Z", j), C1("Cc", 112 * j + 111)) for j in range(K - 1)])
+        group([(ZZ, W("I112"), R("q16", 0, 112))], stop=False)
+        group([(TT, W("I2"), R("q16", 0, 112))] + [(TT, W("I2"), blk("Y", j)) for j in range(K)])
+        group([(ZZ, W("I112"), blk("Y", j)) for j in range(K)], start=False, stop=False)
+        if r == 0:
+            digits(3)
         ts(R("qb", 0, 112), TT, 1.0 / 32, ALU.mult, 136.0 - 17.0 / 32, ALU.add)
         tt(R("Lb", 0, 112), TT, R("q16", 0, 112), ALU.is_le)
         group([(ZZ, W("Iv"), R("qb", 0, 112)), (ZZ, W("Ib"), R("qb", 0, 112)), (ZZ, W("I56"), R("Lb", 0, 112))], start=False)
+        group([(R("pE", 64, 65), RS("Z", j), C1("Cc", 112 * j + 111)) for j in range(K - 1)])
         ts(R("OFF", 0, 112), ZZ, 1791.0 * 136 - 112 + 0.25, ALU.add)
         kv = KV[r]
         act(IND(R("WS%d" % r, 0, V), R("OFF", kv, 112)), R(PAY, 16 * kv, V), AF.Silu)
-        cp(IND(R("WV%d" % r, 0, V), R("OFF", 0, kv)), R(PAY, 0, 16 * kv))
-        dma("y", R("wv", 0, 112), R("WV%d" % r, 0, V, row=0), "wv%d" % r)
+        cp(IND(R("WV", 0, V), R("OFF", 0, kv)), R(PAY, 0, 16 * kv))
+        dma("y", R("wv", 0, 112), R("WV", 0, V, row=0), "wv%d" % r)
         dma("s", R("ws", 0, 112), R("WS%d" % r, 0, V, row=0), "ws%d" % r)
         if r == 0:
             for j, ps in enumerate(("p1", "p2", "p0", "pB")):
@@ -436,24 +438,28 @@ def rank_program(g, core, T, topo):
         send("A", r)
         if r == 0:
             places(1)
-            ts(R("t16", 0, 58), R("tr", 0, 58), C1("col", 0), ALU.subtract)
-            ts(R("tau2", 0, 112), R("tau0", 0, 112), 2.0, ALU.mult, 0.5, ALU.add)
         for j in range(K - 1):
             ts(R("Pj", 64 * j, 64 * j + 58), R("t16", 0, 58), C1("bb", j), ALU.is_ge, C1("td", 8 + j), ALU.mult)
         group([(R("pG", 128, 186), W("Ih"), R("Pj", 64 * j, 64 * j + 58)) for j in range(K - 1)]
               + [(R("pG", 128, 186), W("Ih"), R("t16", 0, 58))])
-        for j in range(K - 1):
-            ts(blk("Oj", j), R("tau2", 0, 112), 0.5, ALU.mult, C1("pC", 128 + j), ALU.is_lt)
+        def olds():
+            for j in range(K - 1):
+                ts(blk("Oj", j), R("tau2", 0, 112), 0.5, ALU.mult, C1("pC", 128 + j), ALU.is_lt)
+
         if r == 0:
+            cp(R("H0", 128, 1920), R("Hi", 0, V))
+            tt(R("ORD", 0, 112), R("wv", 0, 112), R("ws", 0, 112), ALU.max)
+            cp(R("zi", 0, 58), R("pG", 128, 186))
+            cp(R("UL", 0, 112), R("ORD", 0, 112))
+            ts(R("za", 0, 58), R("zi", 0, 58), 1, ALU.bitwise_and)
+            ts(R("tau2", 0, 112), R("tau0", 0, 112), 2.0, ALU.mult, 0.5, ALU.add)
             tt(R("Z2", 0, 144), R("Za", 0, 144), R("Z", 0, 144), ALU.subtract)
-        cp(R("zi", 0, 58), R("pG", 128, 186))
-        if r == 0:
-            cp(R("H0", 128, 1024), R("Hi", 0, M))
-        ts(R("za", 0, 58), R("zi", 0, 58), 1, ALU.bitwise_and)
-        if r == 0:
-            cp(R("H0", 1024, 1920), R("Hi", M, V))
-        tt(R("ORD", 0, 112), R("wv", 0, 112), R("ws", 0, 112), ALU.max)
-        cp(R("UL", 0, 112), R("ORD", 0, 112))
+        else:
+            olds()
+            cp(R("zi", 0, 58), R("pG", 128, 186))
+            ts(R("za", 0, 58), R("zi", 0, 58), 1, ALU.bitwise_and)
+            tt(R("ORD", 0, 112), R("wv", 0, 112), R("ws", 0, 112), ALU.max)
+            cp(R("UL", 0, 112), R("ORD", 0, 112))
         for (o, a, n) in ((0, 46, 10), (10, 0, 48)):
             group([(R("pA", 256 + o, 256 + o + n), W("SH"), R("ORD", 56 + a, 56 + a + n)),
                    (R("pA", 256 + o, 256 + o + n), W("W1"), R("ORD", 55 + a, 55 + a + n))])
@@ -466,59 +472,82 @@ def rank_program(g, core, T, topo):
 
         his(46, 56)
         his(0, 10)
-        tt(R("dm", 0, 58), R("pA", 256, 314), R("za", 0, 58), ALU.mult)
-        his(10, 28)
-        his(28, 46)
+        his(10, 32)
+        his(32, 46)
         gat("Xu", 0, Xw, "UL", 48, 56)
         gat("Xu", 128, Xw, "UL", 0, 8)
-        gat("Xu", 256, Xw, "UL", 8, 48)
+        if last:
+            gat(Nn, 128, Nw, "UL", 0, 8)
         cmpq(0, 46, 56)
         cmpq(160, 0, 10)
         mets("pE", 0, 20, True)
-        cmpq(320, 10, 28)
+        tt(R("dm", 0, 58), R("pA", 256, 314), R("za", 0, 58), ALU.mult)
+        if r == 0:
+            olds()
+        cmpq(320, 10, 32)
         tt(R("Dd", 0, 20), R("pE", 0, 20), R("dm", 0, 20), ALU.max)
         group([(R("pE", 32, 48), W("IU"), R("Dd", 2, 18)), (R("pE", 32, 40), W("Ih"), R("ORD", 104, 112)),
                (R("pE", 40, 48), W("Ih"), R("ORD", 56, 64)), (R("pE", 32, 48), W("W2"), R("Dd", 3, 19))])
-        cmpq(608, 28, 48)
+        cmpq(672, 32, 48)
         mets("pG", 20, 38, False)
         cp(R("LP", 0, 16), R("pE", 32, 48))
+        if last:
+            gat(Nn, 1792, Nw, "LP", 0, 8)
+            send("N", r)
+        gat("Xu", 256, Xw, "UL", 8, 48)
         tt(R("Dx", 0, 256), IND(Xw, R("LP", 0, 16)), R("Xu", 0, 256), ALU.subtract)
         ts(R("Sg", 0, 256), R("Dx", 0, 256), 1.0, ALU.min, -1.0, ALU.max)
         send("S", r)
-        if last:
-            gat(Nn, 128, Nw, "UL", 0, 8)
-            gat(Nn, 1792, Nw, "LP", 0, 8)
         tt(R("Dd", 20, 58), R("pG", 0, 38), R("dm", 20, 58), ALU.max)
         group([(R("pG", 64, 104), W("IU"), R("Dd", 18, 58)), (R("pG", 64, 104), W("Ih"), R("ORD", 64, 104)),
                (R("pG", 64, 103), W("W2"), R("Dd", 19, 58)), (R("pG", 103, 104), W("W2"), R("Dd", 2, 3))])
         ts(R("Gt", 0, 256), R("Dx", 0, 256), 0.0, ALU.is_gt)
         up("p0", 0, 128, 128)
         low("p0", 128, 0, 128)
-        cp(R("LP", 16, 56), R("pG", 64, 104))
         if last:
-            tt(R(Xn, 896, 1024), R("Xu", 0, 128), R("Gt", 0, 128), ALU.add)
+            gat(Nn, 256, Nw, "UL", 8, 28)
         else:
             gat(Nn, 128, Nw, "UL", 0, 56)
+        cp(R("LP", 16, 56), R("pG", 64, 104))
         act(R(Xn, 128, 256), R("p0", 0, 128), AF.Copy)
         act(R(Xn, 1792, 1920), R("p0", 128, 256), AF.Copy)
         send("X", r)
-        if last:
-            send("N", r)
         row = 15 - r
         AI, SI = "AI%d" % r, "SI%d" % r
+        it = [(R("pE", 256, 368), W("Ib"), blk("Oj", j)) for j in range(K - 1)]
+        if last:
+            it.append((R("pE", 256, 368), W("Ib"), R("one", 0, 112)))
+        if prev:
+            it += [(R("pE", 256, 368), RS("Z", 0), R(AI, 0, 112)), (R("pE", 256, 272), RS("Z", 1), R(AI, 112, 128))]
+        if nxt:
+            it += [(R("pE", 352, 368), RS("Z", 14), R(AI, 128, 144)), (R("pE", 256, 368), RS("Z", 15), R(AI, 144, 256))]
+        group(it)
+
+        def play(a, b):
+            tt(R("Dx", 16 * a, 16 * b), IND(Xw, R("LP", a, b)), R("Xu", 16 * a, 16 * b), ALU.subtract)
+            ts(R("Sg", 16 * a, 16 * b), R("Dx", 16 * a, 16 * b), 1.0, ALU.min, -1.0, ALU.max)
+            ts(R("Gt", 16 * a, 16 * b), R("Dx", 16 * a, 16 * b), 0.0, ALU.is_gt)
+
         if last:
             low("p1", 0, 128, 128)
-        it = [(R("pA", 128, 240), W("Ib"), blk("Oj", j)) for j in range(K - 1)]
-        if last:
-            it.append((R("pA", 128, 240), W("Ib"), R("one", 0, 112)))
-        if prev:
-            it += [(R("pA", 128, 240), RS("Z", 0), R(AI, 0, 112)), (R("pA", 128, 144), RS("Z", 1), R(AI, 112, 128))]
-        if nxt:
-            it += [(R("pA", 224, 240), RS("Z", 14), R(AI, 128, 144)), (R("pA", 128, 240), RS("Z", 15), R(AI, 144, 256))]
-        group(it)
-        tt(R("Dx", 256, M), IND(Xw, R("LP", 16, 56)), R("Xu", 256, M), ALU.subtract)
-        ts(R("Sg", 256, M), R("Dx", 256, M), 1.0, ALU.min, -1.0, ALU.max)
-        ts(R("Gt", 256, M), R("Dx", 256, M), 0.0, ALU.is_gt)
+            gat(Nn, 576, Nw, "UL", 28, 56)
+            play(16, 36)
+            low("p1", 128, 256, 320)
+            tt(R(Xn, 256, 576), R("Xu", 256, 576), R("Gt", 256, 576), ALU.add)
+            dma("y", EXT(T.yx[:, 128:448]), R(Xn, 256, 576), "o4")
+            act(R(Xn, 1024, 1472), R("p1", 0, 448), AF.Copy)
+            dma("y", EXT(T.yx[:, 896:1344]), R(Xn, 1024, 1472), "o6")
+            gat(Nn, 1024, Nw, "LP", 8, 56)
+            dma("s", EXT(T.yn[:, 128:1664]), R(Nn, 256, 1792, row=0), "o1")
+            tt(R(Xn, 896, 1024), R("Xu", 0, 128), R("Gt", 0, 128), ALU.add)
+            play(36, 56)
+            low("p2", 0, 576, 320)
+            tt(R(Xn, 576, 896), R("Xu", 576, M), R("Gt", 576, M), ALU.add)
+            dma("y", EXT(T.yx[:, 448:896]), R(Xn, 576, 1024), "o8")
+            cp(R(Xn, 1472, 1792), R("p2", 0, 320))
+            dma("y", EXT(T.yx[:, 1344:1664]), R(Xn, 1472, 1792), "o7")
+        else:
+            play(16, 56)
 
         def wl(i, only_low):
             return RS("Z", 8 + i) if only_low else RS("Z2", i)
@@ -532,30 +561,17 @@ def rank_program(g, core, T, topo):
         it += [(R("pA", 0, 112), RS("Z2", i), R("Sg", 128 + 112 * i, 240 + 112 * i)) for i in range(2, 6)]
         it += [(R("pA", 0, 96), RS("Z2", 6), R("Sg", 800, M))]
         group(it, stop=False)
-        if last:
-            low("p1", 128, 256, 320)
-            low("p2", 0, 576, 320)
-        else:
-            up("p1", 0, 256, 512)
         it = []
         if prev:
             it += [(R("pA", 0, 112), RS("Z", 0), R(SI, 0, 112)), (R("pA", 0, 16), RS("Z", 1), R(SI, 112, 128))]
         if nxt:
             it += [(R("pA", 96, 112), RS("Zn", 14), R(SI, 128, 144)), (R("pA", 0, 112), RS("Zn", 15), R(SI, 144, 256))]
         group(it, start=False)
-        if last:
-            tt(R(Xn, 256, 896), R("Xu", 256, M), R("Gt", 256, M), ALU.add)
-            dma("y", EXT(T.yx[:, 128:896]), R(Xn, 256, 1024), "o4")
-            gat(Nn, 256, Nw, "UL", 8, 56)
-            gat(Nn, 1024, Nw, "LP", 8, 56)
-            dma("s", EXT(T.yn[:, 128:1664]), R(Nn, 256, 1792, row=0), "o1")
-            act(R(Xn, 1024, 1472), R("p1", 0, 448), AF.Copy)
-            dma("s", EXT(T.yx[:, 896:1344]), R(Xn, 1024, 1472), "o6")
-            cp(R(Xn, 1472, 1792), R("p2", 0, 320))
-            dma("y", EXT(T.yx[:, 1344:1664]), R(Xn, 1472, 1792), "o7")
+        if not last:
+            up("p1", 0, 256, 512)
         ts(R("cl", 0, 112), R("pA", 0, 112), 1.0, ALU.min, -1.0, ALU.max)
         if not last:
-            tt(R("sp", 0, 112), R("cl", 0, 112), R("pA", 128, 240), ALU.add)
+            tt(R("sp", 0, 112), R("cl", 0, 112), R("pE", 256, 368), ALU.add)
             gat(Nn, 1792, Nw, "LP", 0, 8)
             send("N", r)
             gat(Nn, 1024, Nw, "LP", 8, 56)
@@ -566,13 +582,13 @@ def rank_program(g, core, T, topo):
             send("H", r)
             zero(r + 1)
         else:
-            tt(R("so", 0, 112), R("cl", 0, 112), R("pA", 128, 240), ALU.add)
+            tt(R("so", 0, 112), R("cl", 0, 112), R("pE", 256, 368), ALU.add)
             a, b = (0 if prev else 128), (1920 if nxt else 1792)
+            dma("s", EXT(T.yx[:, 0:128]), R(Xn, a, a + E), "o5")
+            dma("s", EXT(T.yx[:, 1664:V]), R(Xn, b, b + E), "o5")
             dma("s", EXT(T.yn[:, 0:128]), R(Nn, a, a + E, row=0), "o2")
             dma("s", EXT(T.yn[:, 1664:V]), R(Nn, b, b + E, row=0), "o2")
             dma("y", EXT(T.ys[:]), R("so", 0, 112), "o3")
-            dma("s", EXT(T.yx[:, 0:128]), R(Xn, a, a + E), "o5")
-            dma("s", EXT(T.yx[:, 1664:V]), R(Xn, b, b + E), "o5")
 
     emit(g, T, ops)
 

from concourse.bass import DstId, RemoteDMATransfer
from concourse.mybir import AluOpType as ALU, ActivationFunctionType as AF

V, M, E, RO = 1792, 896, 128, 3
F, B, H, I, U = "float32", "bfloat16", "float16", "int32", "uint16"
KV = [50, 56, 56]
SCRATCH = {}


def _sb(name, cols, dt):
    SCRATCH[name] = ("sbuf", [128, cols], dt)


for _r in range(4):
    _sb("X%d" % _r, 2048, B)
    _sb("N%d" % _r, 2048, F)
    _sb("H%d" % _r, 2048, F)
for _r in range(3):
    _sb("WS%d" % _r, V, F)
    _sb("SI%d" % _r, 256, B)
    _sb("AI%d" % _r, 256, B)
for _n, _c, _d in [
        ("WV", V, F), ("Hi", V, I), ("P0", V, F), ("P1", V, F), ("sci", 112, I), ("nmi", 112, I), ("nr", 112, F), ("dg", 336, B), ("NR", V, B),
        ("zer", 112, F), ("zr2", 112, F), ("one", 112, B), ("m256", 8, B), ("cA", 32, B),
        ("J", 144, B), ("D0", 128, B), ("pc", 8, I), ("pa", 8, I), ("col", 24, F), ("ta", 144, F),
        ("le", 16, F), ("ge", 16, F),
        ("ON", 128, B), ("Oh", 128, B), ("On", 128, B), ("Om", 128, B), ("oa", 128, B), ("ob", 128, B), ("Sel", 128, B),
        ("LT", 128, B), ("UT", 128, B), ("Ib", 128, B), ("In", 128, B), ("Ik", 128, B), ("Iv", 128, B), ("I56", 128, B), ("I112", 128, H),
        ("Z", 144, B), ("Zn", 144, B), ("Za", 144, B), ("Z2", 144, B), ("Z3", 144, B), ("Zm", 144, B), ("Z3m", 144, B),
        ("Ih", 128, H), ("I2", 128, H), ("SH", 128, H), ("W1", 128, H), ("IU", 128, H), ("W2", 128, H),
        ("h1", 128, H), ("h2", 128, H),
        ("tau0", 112, F), ("tau", 112, F), ("tau2", 112, H), ("taur", 256, F), ("tr", 64, F), ("t16", 64, H),
        ("Ec", 896, B), ("Cc", 896, B), ("Mc", 896, H), ("Y", 896, H), ("q16", 112, H), ("qb", 112, B), ("Lb", 112, B),
        ("bb", 32, F), ("td", 16, F), ("OFF", 112, U),
        ("wv", 112, F), ("ws", 112, F), ("UL", 112, U), ("ORD", 112, H),
        ("Pj", 512, H), ("Oj", 896, B), ("A", 256, B), ("zi", 64, I), ("za", 64, I), ("dm", 64, H),
        ("EQ", 928, B), ("Dd", 64, H), ("LP", 56, U),
        ("Xu", M, B), ("Dx", M, B), ("Sg", M, B), ("Gt", M, B), ("cl", 112, B), ("sp", 112, B), ("so", 112, F)]:
    _sb(_n, _c, _d)
PSUM = ["pA", "pB", "pC", "pE", "pG", "p0", "p1", "p2"]
for _n in PSUM:
    SCRATCH[_n] = ("psum", [128, 512], F)

KINDS = ["A", "S", "X", "N", "H"]
SEMAPHORES = ["qv", "qs", "qt", "qg", "lsc", "lnm", "lx", "lh", "lnd", "o1", "o2", "o3", "o4", "o5", "o6", "o7", "o8"]
for _r in range(RO):
    SEMAPHORES += ["wv%d" % _r, "ws%d" % _r, "im%d" % _r, "lz%d" % _r]
    for _k in KINDS:
        SEMAPHORES += ["a%s%d" % (_k, _r), "l%s%d" % (_k, _r)]

MAGIC = 12582912.0
BIG = 4096.0


def pieces(kind, r):
    if kind == "A":
        return ("A", 128, 0, "AI%d" % r, 128, 0)
    if kind == "S":
        return ("Sg", 128, 0, "SI%d" % r, 128, 0)
    n = "%s%d" % (kind, r + 1)
    return (n, 128, 1792, n, 1920, 0)


def relays(T, topo, rank):
    core = T.cores[rank]
    out, used = {}, []
    for d, nb in ((0, rank - 1), (1, rank + 1)):
        if nb < 0 or nb >= len(T.cores):
            continue
        ok = [c for c in topo.cores_of(core) if c != core and c not in used and topo.may_write(c, T.cores[nb])]
        near = [c for c in ok if topo.die(c) == topo.die(core)][0]
        far = [c for c in ok if topo.die(c) != topo.die(core)][0]
        used += [near, far]
        out[d] = (near, far)
    return out


def relay_of(kind, pair):
    return pair[0] if kind in ("A", "S", "X") else pair[1]


def half_mask(topo, src, dst, d):
    e = topo.engines(src, dst)
    h = len(e) // 2
    return sum(1 << x for x in (e[:h] if d == 0 else e[h:])), h


def relay_program(g, core, T, topo):
    for rank in range(len(T.cores)):
        for d, pair in relays(T, topo, rank).items():
            if core not in pair:
                continue
            dst = T.cores[rank - 1 if d == 0 else rank + 1]
            rid, pid = topo.addr(dst, core)
            n_in = half_mask(topo, T.cores[rank], core, d)[1]
            n_out = len(topo.engines(core, dst))
            done = []
            for r in range(RO):
                for k in KINDS:
                    if relay_of(k, pair) != core or (k == "H" and r == RO - 1):
                        continue
                    p = pieces(k, r)
                    ap = T[p[3]][:, p[4 + d]:p[4 + d] + E]
                    g.wait_ge(T.sem["a%s%d" % (k, r)], n_in)
                    g.remote_dma(ap, ap, T.sem["a%s%d" % (k, r)], T.sem["l%s%d" % (k, r)], pid, rid, topo.mask(core, dst))
                    done.append("l%s%d" % (k, r))
            for s in done:
                g.wait_ge(T.sem[s], n_out)


def rank_program(g, core, T, topo):
    rank = T.rank_of(core)
    if rank is None:
        relay_program(g, core, T, topo)
        return
    prev, nxt = rank > 0, rank < len(T.cores) - 1
    rel = relays(T, topo, rank)
    ops = []

    def R(name, a, b, step=None, row=None, part=None):
        t = T[name]
        if row is not None:
            ap = t[row:128:16, a:b]
        elif part is not None:
            ap = t[part[0]:part[1], a:b]
        elif step is not None:
            ap = t[:, a:b:step]
        else:
            ap = t[:, a:b]
        return (ap, [(name, a, b)], [])

    def IND(win, off):
        return (win[0].indirect(off[0]), win[1], off[1])

    def EXT(ap):
        return (ap, [], [])

    def add(q, fn, outs, ins, sem=None, inc=16):
        rd, wr = [], []
        for o in outs:
            wr += o[1]
            rd += o[2]
        for x in ins:
            if isinstance(x, tuple):
                rd += x[1] + x[2]
        ops.append({"q": q, "fn": fn, "rd": rd, "wr": wr, "sem": sem, "inc": inc})

    def val(x):
        return x[0] if isinstance(x, tuple) else x

    def fill(out, c):
        add("v", lambda: g.vector.memset(out[0], c), [out], [])

    def ts(out, a, s1, op0, s2=None, op1=None):
        if op1 is None:
            add("v", lambda: g.vector.tensor_scalar(out[0], a[0], val(s1), None, op0), [out], [a, s1])
        else:
            add("v", lambda: g.vector.tensor_scalar(out[0], a[0], val(s1), val(s2), op0, op1), [out], [a, s1, s2])

    def tt(out, a, b, op):
        add("v", lambda: g.vector.tensor_tensor(out[0], a[0], b[0], op), [out], [a, b])

    def cp(out, a):
        add("v", lambda: g.vector.tensor_copy(out[0], a[0]), [out], [a])

    def scan(a, b, first):
        x, o = R("Ec", a, b), R("Cc", a, b)
        add("v", lambda: g.vector.tensor_tensor_scan(o[0], x[0], x[0], val(first), ALU.add, ALU.max), [o], [x, first])

    def act(out, a, func, bias=None, scale=None):
        kw = {}
        if bias is not None:
            kw["bias"] = val(bias)
        if scale is not None:
            kw["scale"] = val(scale)
        add("s", lambda: g.scalar.activation(out[0], a[0], func, **kw), [out], [a, bias, scale])

    def lin(out, a, scale, bias):
        act(out, a, AF.Identity, bias=bias, scale=scale)

    def group(items, start=True, stop=True):
        for n, (out, l, rr) in enumerate(items):
            add("t", lambda out=out, l=l, rr=rr, n=n: g.tensor.matmul(out[0], l[0], rr[0], start and n == 0,
                                                                      stop and n == len(items) - 1), [out], [l, rr])

    def iota(out, pat, base, cm, isint=False):
        if isint:
            add("g", lambda: g.iota(out[0], pat, base, cm), [out], [])
        else:
            add("g", lambda: g.iota(out[0], pat, base, cm, allow_small_or_imprecise_dtypes=True), [out], [])

    def dma(q, out, a, sem):
        eng = g.sync if q == "y" else g.scalar
        add(q, lambda: eng.dma_start(out[0], a[0]), [out], [a], sem=sem)

    def send(kind, r):
        p = pieces(kind, r)
        trs, srcs, tot, got, lands = [], [], 0, 0, []
        for d in sorted(rel):
            h = relay_of(kind, rel[d])
            rid, pid = topo.addr(h, core)
            m, n = half_mask(topo, core, h, d)
            s = R(p[0], p[1 + d], p[1 + d] + E)
            srcs.append(s)
            trs.append(RemoteDMATransfer(dst_ids=[DstId(rid=rid, pnc=pid)], dma_engine_mask=m, remote_sem=T.sem["a%s%d" % (kind, r)],
                                         src=s[0], dst=T[p[3]][:, p[4 + d]:p[4 + d] + E]))
            tot += n
            nb = rank - 1 if d == 0 else rank + 1
            far = relay_of(kind, relays(T, topo, nb)[1 - d])
            got += len(topo.engines(far, core))
            lands.append(R(p[3], p[5 - d], p[5 - d] + E))
        ls = "l%s%d" % (kind, r)
        add("g", lambda: g.remote_dma_fused(trs, local_sem=T.sem[ls]), [], srcs, sem=ls, inc=tot)
        ops[-1]["own"] = True
        add("x", None, lands, [], sem="a%s%d" % (kind, r), inc=got)

    def RS(name, i):
        return R(name, 15 - i, 143 - i)

    def C1(name, j):
        return R(name, j, j + 1)

    def W(name):
        return R(name, 0, 128)

    def blk(name, j):
        return R(name, 112 * j, 112 * j + 112)

    def zero(r):
        dma("y", R("WV", 0, V, row=0), R("zer", 0, 112), "lz%d" % r)
        dma("y", R("WS%d" % r, 0, V, row=0), R("zr2" if r else "zer", 0, 112), "lz%d" % r)

    def sel(out, a, op, c, base, sign=1):
        add("g", lambda: g.affine_select(T[out][:], T[a][:], [[sign, 128]], op, c, base, -sign), [W(out)], [W(a)])

    def hat(name, c, k):
        act(R("ta", 0, 144), R("J", 0, 144), AF.Abs, bias=C1("col", c))
        act(R(name, 0, 144), R("ta", 0, 144), AF.Relu, bias=k, scale=-1.0)

    dma("y", R("sci", 0, 112), EXT(T.sc[:]), "lsc")
    dma("s", R("nmi", 0, 112), EXT(T.nm[:]), "lnm")
    fill(R("zer", 0, 112), 0.0)
    zero(0)
    dma("y", R("Hi", 0, V), EXT(T.hi[:]), "lh")
    iota(R("pc", 0, 1), [[1, 1]], 0, 1, True)
    iota(R("J", 0, 144), [[1, 144]], 0, 0)
    iota(R("tau", 0, 112), [[1, 112]], 0, 112)
    iota(R("tr", 0, 10), [[16, 10]], 16 * 46, 1)
    iota(R("tr", 10, 58), [[16, 48]], 0, 1)
    iota(R("P0", 0, V), [[1, 112], [112, 16]], 0, 0)
    act(R("zr2", 0, 112), R("zer", 0, 112), AF.Silu)
    fill(R("m256", 0, 8), -BIG / 16)
    ts(R("pa", 0, 1), R("pc", 0, 1), 112, ALU.bitwise_and)
    ts(R("pa", 1, 2), R("pc", 0, 1), 7, ALU.bitwise_and)
    cp(C1("col", 16), R("pc", 0, 1))
    fill(R("cA", 0, 8), -1.0 / 64)
    cp(C1("col", 0), R("pa", 0, 1))
    ts(C1("col", 17), R("pa", 1, 2), -16.0, ALU.mult, -7.5, ALU.add)
    fill(R("cA", 8, 16), 1.0 / 64)
    fill(R("cA", 16, 32), -1.0 / 64)
    ts(W("D0"), W("J"), C1("col", 16), ALU.subtract)
    ts(W("oa"), W("J"), C1("col", 0), ALU.subtract, 0.0, ALU.is_ge)
    ts(W("ob"), W("J"), C1("col", 0), ALU.subtract, 16.0, ALU.is_lt)
    ts(W("Ib"), W("D0"), 0.0, ALU.is_equal)
    ts(W("LT"), W("D0"), 0.0, ALU.is_gt)
    ts(W("UT"), W("D0"), 0.0, ALU.is_lt)
    tt(W("ON"), W("oa"), W("ob"), ALU.mult)
    ts(W("Ik"), W("D0"), 0.0, ALU.is_equal, BIG, ALU.mult)
    tt(W("LT"), W("LT"), W("ob"), ALU.mult)
    tt(W("UT"), W("UT"), W("oa"), ALU.mult)
    tt(C1("col", 1), R("pc", 0, 1), R("pa", 0, 1), ALU.subtract)
    lin(W("Oh"), W("ON"), 0.5, 0.0)
    lin(W("On"), W("ON"), -0.5, 0.0)
    act(R("ta", 0, 128), W("J"), AF.Abs, bias=C1("col", 17))
    act(W("Sel"), R("ta", 0, 128), AF.Sign, bias=8.0, scale=-1.0)
    for j, sc_, bi_ in ((2, -1.0, -15.0), (3, -1.0, -23.0), (4, -1.0, -15.5), (7, -112.0, -895.75)):
        lin(C1("col", j), C1("col", 0), sc_, bi_)
    act(W("Sel"), W("Sel"), AF.Relu)
    hat("Z", 2, 1.0)
    lin(W("Om"), W("ON"), -1.0, 0.0)
    lin(W("Iv"), W("Ib"), -1792.0, 0.0)
    lin(W("I56"), W("Ib"), 56.0, 0.0)
    iota(R("taur", 0, 128), [[2, 128]], 2 * 768 + 1, 0)
    iota(R("taur", 128, 256), [[2, 128]], 0, 0)
    sel("h1", "ON", ALU.is_equal, 0.0, -1)
    sel("W1", "ON", ALU.is_equal, 0.0, 15)
    sel("SH", "h1", ALU.not_equal, -1.0, 0)
    sel("h2", "Om", ALU.is_equal, 0.0, 1)
    sel("W2", "Om", ALU.is_equal, 0.0, -15)
    sel("IU", "h2", ALU.not_equal, 1.0, 0)
    lo1 = 0 if prev else 128

    def places(half):
        iota(R("P1", M * half, M * half + M), [[1, 56], [112, 16]], 128 - lo1 + 56 * half, 0)
        if half and prev:
            iota(R("P1", 0, V, step=16), [[1, 112]], 0, 0)
            iota(R("P1", 1, 256, step=16), [[1, 16]], 112, 0)
        if half and nxt:
            iota(R("P1", 96 * 16 + 14, V, step=16), [[1, 16]], 1664 + 256 - lo1, 0)
            iota(R("P1", 15, V, step=16), [[1, 112]], 1680 + 256 - lo1, 0)
        if half:
            iota(R("one", 0, 112), [[0, 112]], 1, 0)

    places(0)

    def digits(step):
        if step == 0:
            cp(blk("dg", 0), R("nmi", 0, 112))
        elif step == 1:
            tt(R("nr", 0, 112), R("nmi", 0, 112), blk("dg", 0), ALU.subtract)
        elif step == 2:
            cp(blk("dg", 1), R("nr", 0, 112))
        else:
            tt(blk("dg", 2), R("nr", 0, 112), blk("dg", 1), ALU.subtract)
            for d in range(3):
                dma("y", R("NR", 0, V, part=(8 * d, 8 * d + 8)), blk("dg", d), "lnd")
            dma("y", R("X0", 128, 1920), EXT(T.x[:]), "lx")

    def consts2():
        lin(R("ge", 1, 16), R("le", 0, 15), -1.0, BIG)
        lin(C1("col", 8), C1("le", 7), 895.5 / BIG, C1("col", 7))
        hat("Z3", 4, 1.5)
        parts = ((0, 16, 1, 15), (16, 96, 0, 15), (96, 112, 0, 14))
        cs = [8, 8, 8]
        for on, name, k, c0 in ((prev, "le", 2, 9), (nxt, "ge", 3, 12)):
            for j, p in enumerate(parts if on else ()):
                lin(C1("col", c0 + j), C1(name, p[k]), 1.0, C1("col", cs[j]))
                cs[j] = c0 + j
            lin(R("Zm" if k == 2 else "Zn", 0, 144), R("Z", 0, 144), -2048.0 if k == 2 else -1.0, 0.0)
        hat("Za", 3, 1.0)
        for j, p in enumerate(parts):
            lin(R("tau0", p[0], p[1]), R("tau", p[0], p[1]), 1.0, C1("col", cs[j]))
        lin(R("Z3m", 0, 144), R("Z3", 0, 144), -2048.0, 0.0)
        lin(W("In"), W("Ib"), -1.0, 0.0)

    def up(ps, o, c, n):
        group([(R(ps, o, o + n), W("Ib"), R("Xu", c, c + n)), (R(ps, o, o + n), W("Ib"), R("Gt", c, c + n))])

    def low(ps, o, c, n):
        group([(R(ps, o, o + n), W("Ib"), R("Xu", c, c + n)), (R(ps, o, o + n), W("Ib"), R("Dx", c, c + n)),
               (R(ps, o, o + n), W("In"), R("Sg", c, c + n)), (R(ps, o, o + n), W("Ib"), R("Gt", c, c + n))])

    def gat(dst, c0, win, off, a, b):
        act(R(dst, c0, c0 + 16 * (b - a)), IND(win, R(off, a, b)), AF.Copy)

    def mets(ps, c0, n, first):
        it = [(R(ps, 0, n), RS("Z3m", i), R("EQ", 16 * c0 + i, 16 * (c0 + n), step=16)) for i in range(15)]
        if first:
            it.append((R(ps, 1, n), RS("Zm", 0), R("EQ", 15, 16 * (n - 1), step=16)))
        else:
            it.append((R(ps, 0, n), RS("Zm", 0), R("EQ", 16 * c0 - 1, 16 * (c0 + n - 1), step=16)))
        it.append((R(ps, 0, n), RS("Zm", 15), R("EQ", 16 * c0 + 15, 16 * (c0 + n), step=16)))
        group(it)

    for r in range(RO):
        K = 4 + 2 * r
        K2 = K // 2
        last = r == RO - 1
        lo, hi = (128, 1920) if r == 0 else (lo1, 2048 if nxt else 1920)
        Xc, Xn, Nn, Hn = "X%d" % r, "X%d" % (r + 1), "N%d" % (r + 1), "H%d" % (r + 1)
        Xw, Nw, Hw = R(Xc, lo, hi), R("N%d" % r, lo, hi), R("H%d" % r, lo, hi)
        PAY = "P0" if r == 0 else "P1"
        Wd = 112 * K
        group([(R("pC", 128, 160), W("ON"), R("cA", 0, 32))], stop=False)
        for ps, pb, a in (("p2", "pB", 0), ("p0", "pE", K2)):
            b = a + K2
            for j in range(a + 1 if a else 0, min(b + 1, K)):
                k = K - 1 - j
                if r == 0:
                    ts(blk("Ec", j), R("sci", 0, 112), float(k), ALU.is_equal)
                else:
                    ts(blk("Ec", j), R("sp", 0, 112), float(k - 1), ALU.is_equal)
            if r == 0 and a:
                digits(0)
            group([(R(ps, 0, 112 * K2), W("Ik"), R("Ec", 112 * a, 112 * b))], stop=False)
            scan(112 * a, 112 * b, C1("Cc", 112 * a - 1) if a else 0.0)
            a1 = max(a, 1)
            group([(R(pb, 128 + a, 128 + b), W("ON"), R("m256", a, b)),
                   (R(pb, 128 + a, 128 + b), W("LT"), R("Cc", 112 * a + 111, 112 * b, step=112)),
                   (R(pb, 128 + a1, 128 + b), W("UT"), R("Cc", 112 * a1 - 1, 112 * (b - 1), step=112))])
            group([(R(ps, 0, 112 * K2), W("Ib"), R("Cc", 112 * a, 112 * b))], start=False)
        hiK, hiJ = R("Cc", 111, Wd, step=112), R("Cc", 111, Wd - 112, step=112)
        group([(R("pC", 128, 128 + K), W("Oh"), hiK), (R("pC", 136, 136 + K), W("On"), hiK),
               (R("pC", 145, 144 + K), W("Oh"), hiJ), (R("pC", 153, 152 + K), W("Oh"), hiJ)], start=False)
        if r == 0:
            ts(W("Ih"), W("D0"), 0.0, ALU.is_equal)
            ts(R("le", 0, 16), R("J", 0, 16), C1("col", 1), ALU.is_ge, BIG, ALU.mult)
            consts2()
        for j in range(K2):
            ts(blk("Mc", j), blk("p2", j), C1("pB", 128 + j), ALU.add, 0.0, ALU.max)
        if r == 0:
            digits(1)
        for j in range(K2, K):
            if j == K - 1:
                ts(R("bb", 0, 32), R("pC", 128, 160), MAGIC, ALU.add, -MAGIC, ALU.add)
            ts(blk("Mc", j), blk("p0", j - K2), C1("pE", 128 + j), ALU.add, 0.0, ALU.max)
        group([(R("pA", 384, 496), W("Ih"), blk("Mc", j)) for j in range(K)])
        tt(R("td", 0, 16), R("bb", 0, 16), R("bb", 16, 32), ALU.add)
        if r == 0:
            digits(2)
            ts(W("I2"), W("D0"), 0.0, ALU.is_equal, 2.0, ALU.mult)
            ts(W("I112"), W("D0"), 0.0, ALU.is_equal, 112.0, ALU.mult)
        cp(R("q16", 0, 112), R("pA", 384, 496))
        if r == 0:
            ts(R("t16", 0, 58), R("tr", 0, 58), C1("col", 0), ALU.subtract)
        for j in range(K):
            ts(blk("Y", j), R("q16", 0, 112), C1("td", j), ALU.is_gt, C1("td", 8 + j), ALU.mult)
        TT = R("pG", 256, 368)
        ZZ = R("pB", 256, 368)
        group([(ZZ, W("I112"), R("q16", 0, 112))], stop=False)
        group([(TT, W("I2"), R("q16", 0, 112))] + [(TT, W("I2"), blk("Y", j)) for j in range(K)])
        group([(ZZ, W("I112"), blk("Y", j)) for j in range(K)], start=False, stop=False)
        if r == 0:
            digits(3)
        ts(R("qb", 0, 112), TT, 1.0 / 32, ALU.mult, 136.0 - 17.0 / 32, ALU.add)
        tt(R("Lb", 0, 112), TT, R("q16", 0, 112), ALU.is_le)
        group([(ZZ, W("Iv"), R("qb", 0, 112)), (ZZ, W("Ib"), R("qb", 0, 112)), (ZZ, W("I56"), R("Lb", 0, 112))], start=False)
        group([(R("pE", 64, 65), RS("Z", j), C1("Cc", 112 * j + 111)) for j in range(K - 1)])
        ts(R("OFF", 0, 112), ZZ, 1791.0 * 136 - 112 + 0.25, ALU.add)
        kv = KV[r]
        act(IND(R("WS%d" % r, 0, V), R("OFF", kv, 112)), R(PAY, 16 * kv, V), AF.Silu)
        cp(IND(R("WV", 0, V), R("OFF", 0, kv)), R(PAY, 0, 16 * kv))
        dma("y", R("wv", 0, 112), R("WV", 0, V, row=0), "wv%d" % r)
        dma("s", R("ws", 0, 112), R("WS%d" % r, 0, V, row=0), "ws%d" % r)
        if r == 0:
            for j, ps in enumerate(("p1", "p2", "p0", "pB")):
                group([(R(ps, 0, 448), R("Sel", 0, 128, part=(0, 24)), R("NR", 448 * j, 448 * j + 448, part=(0, 24)))])
                act(R("N0", 128 + 448 * j, 576 + 448 * j), R(ps, 0, 448), AF.Copy)
        else:
            up("p2", 0, 768, 128)
            up("p2", 128, 0, 128)
            low("p2", 256, 128, 256)
            low("p0", 0, 384, 512)
            act(R(Xc, 256, 768), R("p1", 0, 512), AF.Copy)
            act(R(Xc, 768, 1280), R("p2", 0, 512), AF.Copy)
            act(R(Xc, 1280, 1792), R("p0", 0, 512), AF.Copy)
        ts(R("A", 0, 256), R("taur", 0, 256), C1("pE", 64), ALU.is_lt)
        send("A", r)
        if r == 0:
            places(1)
        for j in range(K - 1):
            ts(R("Pj", 64 * j, 64 * j + 58), R("t16", 0, 58), C1("bb", j), ALU.is_ge, C1("td", 8 + j), ALU.mult)
        group([(R("pG", 128, 186), W("Ih"), R("Pj", 64 * j, 64 * j + 58)) for j in range(K - 1)]
              + [(R("pG", 128, 186), W("Ih"), R("t16", 0, 58))])
        def olds():
            for j in range(K - 1):
                ts(blk("Oj", j), R("tau2", 0, 112), 0.5, ALU.mult, C1("pC", 128 + j), ALU.is_lt)

        if r == 0:
            cp(R("H0", 128, 1920), R("Hi", 0, V))
            tt(R("ORD", 0, 112), R("wv", 0, 112), R("ws", 0, 112), ALU.max)
            cp(R("zi", 0, 58), R("pG", 128, 186))
            cp(R("UL", 0, 112), R("ORD", 0, 112))
            ts(R("za", 0, 58), R("zi", 0, 58), 1, ALU.bitwise_and)
            ts(R("tau2", 0, 112), R("tau0", 0, 112), 2.0, ALU.mult, 0.5, ALU.add)
            tt(R("Z2", 0, 144), R("Za", 0, 144), R("Z", 0, 144), ALU.subtract)
        else:
            olds()
            cp(R("zi", 0, 58), R("pG", 128, 186))
            ts(R("za", 0, 58), R("zi", 0, 58), 1, ALU.bitwise_and)
            tt(R("ORD", 0, 112), R("wv", 0, 112), R("ws", 0, 112), ALU.max)
            cp(R("UL", 0, 112), R("ORD", 0, 112))
        for (o, a, n) in ((0, 46, 10), (10, 0, 48)):
            group([(R("pA", 256 + o, 256 + o + n), W("SH"), R("ORD", 56 + a, 56 + a + n)),
                   (R("pA", 256 + o, 256 + o + n), W("W1"), R("ORD", 55 + a, 55 + a + n))])

        def cmpq(c0, a, b):
            tt(R("EQ", c0, c0 + 16 * (b - a)), IND(Nw, R("UL", 56 + a, 56 + b)), R(Hn, 128 + 16 * a, 128 + 16 * b), ALU.is_equal)

        def his(a, b):
            gat(Hn, 128 + 16 * a, Hw, "UL", a, b)

        his(46, 56)
        his(0, 10)
        his(10, 32)
        his(32, 46)
        gat("Xu", 0, Xw, "UL", 48, 56)
        gat("Xu", 128, Xw, "UL", 0, 8)
        if last:
            gat(Nn, 128, Nw, "UL", 0, 8)
        cmpq(0, 46, 56)
        cmpq(160, 0, 10)
        mets("pE", 0, 20, True)
        tt(R("dm", 0, 58), R("pA", 256, 314), R("za", 0, 58), ALU.mult)
        if r == 0:
            olds()
        cmpq(320, 10, 32)
        tt(R("Dd", 0, 20), R("pE", 0, 20), R("dm", 0, 20), ALU.max)
        group([(R("pE", 32, 48), W("IU"), R("Dd", 2, 18)), (R("pE", 32, 40), W("Ih"), R("ORD", 104, 112)),
               (R("pE", 40, 48), W("Ih"), R("ORD", 56, 64)), (R("pE", 32, 48), W("W2"), R("Dd", 3, 19))])
        cmpq(672, 32, 48)
        mets("pG", 20, 38, False)
        cp(R("LP", 0, 16), R("pE", 32, 48))
        if last:
            gat(Nn, 1792, Nw, "LP", 0, 8)
            send("N", r)
        gat("Xu", 256, Xw, "UL", 8, 48)
        tt(R("Dx", 0, 256), IND(Xw, R("LP", 0, 16)), R("Xu", 0, 256), ALU.subtract)
        ts(R("Sg", 0, 256), R("Dx", 0, 256), 1.0, ALU.min, -1.0, ALU.max)
        send("S", r)
        tt(R("Dd", 20, 58), R("pG", 0, 38), R("dm", 20, 58), ALU.max)
        group([(R("pG", 64, 104), W("IU"), R("Dd", 18, 58)), (R("pG", 64, 104), W("Ih"), R("ORD", 64, 104)),
               (R("pG", 64, 103), W("W2"), R("Dd", 19, 58)), (R("pG", 103, 104), W("W2"), R("Dd", 2, 3))])
        ts(R("Gt", 0, 256), R("Dx", 0, 256), 0.0, ALU.is_gt)
        up("p0", 0, 128, 128)
        low("p0", 128, 0, 128)
        if last:
            gat(Nn, 256, Nw, "UL", 8, 28)
        else:
            gat(Nn, 128, Nw, "UL", 0, 56)
        cp(R("LP", 16, 56), R("pG", 64, 104))
        act(R(Xn, 128, 256), R("p0", 0, 128), AF.Copy)
        act(R(Xn, 1792, 1920), R("p0", 128, 256), AF.Copy)
        send("X", r)
        row = 15 - r
        AI, SI = "AI%d" % r, "SI%d" % r
        it = [(R("pE", 256, 368), W("Ib"), blk("Oj", j)) for j in range(K - 1)]
        if last:
            it.append((R("pE", 256, 368), W("Ib"), R("one", 0, 112)))
        if prev:
            it += [(R("pE", 256, 368), RS("Z", 0), R(AI, 0, 112)), (R("pE", 256, 272), RS("Z", 1), R(AI, 112, 128))]
        if nxt:
            it += [(R("pE", 352, 368), RS("Z", 14), R(AI, 128, 144)), (R("pE", 256, 368), RS("Z", 15), R(AI, 144, 256))]
        group(it)

        def play(a, b):
            tt(R("Dx", 16 * a, 16 * b), IND(Xw, R("LP", a, b)), R("Xu", 16 * a, 16 * b), ALU.subtract)
            ts(R("Sg", 16 * a, 16 * b), R("Dx", 16 * a, 16 * b), 1.0, ALU.min, -1.0, ALU.max)
            ts(R("Gt", 16 * a, 16 * b), R("Dx", 16 * a, 16 * b), 0.0, ALU.is_gt)

        if last:
            low("p1", 0, 128, 128)
            gat(Nn, 576, Nw, "UL", 28, 56)
            play(16, 36)
            low("p1", 128, 256, 320)
            tt(R(Xn, 256, 576), R("Xu", 256, 576), R("Gt", 256, 576), ALU.add)
            dma("y", EXT(T.yx[:, 128:448]), R(Xn, 256, 576), "o4")
            act(R(Xn, 1024, 1472), R("p1", 0, 448), AF.Copy)
            dma("y", EXT(T.yx[:, 896:1344]), R(Xn, 1024, 1472), "o6")
            gat(Nn, 1024, Nw, "LP", 8, 56)
            dma("s", EXT(T.yn[:, 128:1664]), R(Nn, 256, 1792, row=0), "o1")
            tt(R(Xn, 896, 1024), R("Xu", 0, 128), R("Gt", 0, 128), ALU.add)
            play(36, 56)
            low("p2", 0, 576, 320)
            tt(R(Xn, 576, 896), R("Xu", 576, M), R("Gt", 576, M), ALU.add)
            dma("y", EXT(T.yx[:, 448:896]), R(Xn, 576, 1024), "o8")
            cp(R(Xn, 1472, 1792), R("p2", 0, 320))
            dma("y", EXT(T.yx[:, 1344:1664]), R(Xn, 1472, 1792), "o7")
        else:
            play(16, 56)

        def wl(i, only_low):
            return RS("Z", 8 + i) if only_low else RS("Z2", i)

        def wu(i, only_up):
            return RS("Zn", i) if only_up else RS("Z2", i)

        it = [(R("pA", 0, 112), wl(0, prev), R("Sg", 128, 240)), (R("pA", 0, 16), wl(1, prev), R("Sg", 240, 256)),
              (R("pA", 96, 112), wu(6, nxt), R("Sg", 0, 16)), (R("pA", 0, 112), wu(7, nxt), R("Sg", 16, 128)),
              (R("pA", 16, 112), RS("Z2", 1), R("Sg", 256, 352))]
        it += [(R("pA", 0, 112), RS("Z2", i), R("Sg", 128 + 112 * i, 240 + 112 * i)) for i in range(2, 6)]
        it += [(R("pA", 0, 96), RS("Z2", 6), R("Sg", 800, M))]
        group(it, stop=False)
        it = []
        if prev:
            it += [(R("pA", 0, 112), RS("Z", 0), R(SI, 0, 112)), (R("pA", 0, 16), RS("Z", 1), R(SI, 112, 128))]
        if nxt:
            it += [(R("pA", 96, 112), RS("Zn", 14), R(SI, 128, 144)), (R("pA", 0, 112), RS("Zn", 15), R(SI, 144, 256))]
        group(it, start=False)
        if not last:
            up("p1", 0, 256, 512)
        ts(R("cl", 0, 112), R("pA", 0, 112), 1.0, ALU.min, -1.0, ALU.max)
        if not last:
            tt(R("sp", 0, 112), R("cl", 0, 112), R("pE", 256, 368), ALU.add)
            gat(Nn, 1792, Nw, "LP", 0, 8)
            send("N", r)
            gat(Nn, 1024, Nw, "LP", 8, 56)
            gat(Hn, 1792, Hw, "LP", 0, 8)
            gat(Hn, 1024, Hw, "LP", 8, 56)
            dma("y", R(Hn, 128, 1024, row=row), R(Nn, 1024, 1920, row=0), "im%d" % r)
            dma("y", R(Hn, 1024, 1920, row=row), R(Nn, 128, 1024, row=0), "im%d" % r)
            send("H", r)
            zero(r + 1)
        else:
            tt(R("so", 0, 112), R("cl", 0, 112), R("pE", 256, 368), ALU.add)
            a, b = (0 if prev else 128), (1920 if nxt else 1792)
            dma("s", EXT(T.yx[:, 0:128]), R(Xn, a, a + E), "o5")
            dma("s", EXT(T.yx[:, 1664:V]), R(Xn, b, b + E), "o5")
            dma("s", EXT(T.yn[:, 0:128]), R(Nn, a, a + E, row=0), "o2")
            dma("s", EXT(T.yn[:, 1664:V]), R(Nn, b, b + E, row=0), "o2")
            dma("y", EXT(T.ys[:]), R("so", 0, 112), "o3")

    emit(g, T, ops)


def emit(g, T, ops):
    eng = {"v": g.vector, "s": g.scalar, "t": g.tensor, "g": g, "y": g.sync}
    total, hist = {}, {}
    for o in ops:
        if o["sem"]:
            total[o["sem"]] = total.get(o["sem"], 0) + o["inc"]
    known = {q: {} for q in eng}
    for n, o in enumerate(ops):
        deps = set()
        acc = [(x, False) for x in o["rd"]] + [(x, True) for x in o["wr"]]
        for (name, a, b), w in acc:
            ps = name in PSUM
            for (m, a2, b2, w2) in hist.get(name, []):
                p = ops[m]
                if p["sem"] and p["sem"] == o["sem"]:
                    continue
                if ps:
                    if p["q"] != o["q"]:
                        deps.add(m)
                elif (w or w2) and a < b2 and a2 < b:
                    deps.add(m)
        for (name, a, b), w in acc:
            hist.setdefault(name, []).append((n, a, b, w))
        o["waits"] = []
        if o["q"] == "x":
            o["clock"] = {o["sem"]: 1}
            continue
        kn = known[o["q"]]
        for m in sorted(deps, reverse=True):
            p = ops[m]
            if p["sem"]:
                if p["sem"] in kn:
                    continue
            elif kn.get(p["q"], -1) >= m:
                continue
            o["waits"].append(m)
            p["mark"] = True
            for k, x in p["clock"].items():
                kn[k] = max(kn.get(k, -1), x)
        o["clock"] = dict(kn)
        if o["sem"]:
            o["clock"][o["sem"]] = 1
        else:
            o["clock"][o["q"]] = n
    count = {q: 0 for q in eng}
    for o in ops:
        q = o["q"]
        if q == "x":
            continue
        for m in o["waits"]:
            p = ops[m]
            if p["sem"]:
                eng[q].wait_ge(T.sem[p["sem"]], total[p["sem"]])
            else:
                eng[q].wait_ge(T.sem["q" + p["q"]], p["num"])
        ins = o["fn"]()
        if o["sem"]:
            if not o.get("own"):
                ins.then_inc(T.sem[o["sem"]], 16)
        elif o.get("mark"):
            count[q] += 1
            o["num"] = count[q]
            ins.then_inc(T.sem["q" + q], 1)
    late = [s for s in total if s[0] == "o"]
    for s, n in total.items():
        if s not in late:
            g.wait_ge(T.sem[s], n)
    for q in "tgsv":
        if count[q]:
            g.wait_ge(T.sem["q" + q], count[q])
    for s in late:
        g.wait_ge(T.sem[s], total[s])
